import numpy as np
import ml_dtypes

BF16 = ml_dtypes.bfloat16


def bf(x):
    return np.asarray(x, np.float32).astype(BF16)


def f32(x):
    return np.asarray(x, np.float32)


def f64(x):
    return np.asarray(x).astype(np.float64)


def striped(idx):
    return np.concatenate([l.reshape(-1, 16).T for l in idx])


def rows(idx, k):
    return np.tile(np.repeat(idx, 16, axis=0), (k // (16 * 8), 1))


def look(tab, idx):
    return np.take_along_axis(f64(tab), rows(idx, len(tab)), axis=1)


K, S, D, V, N, M = 128, 2048, 2, 1024, 2048, 128


def setup_inputs():
    return {"tab": f32(np.random.standard_normal((K, S))), "x0": f32(1.0 * np.random.standard_normal((K, V))), "w": bf(np.random.standard_normal((K, M)) / np.sqrt(K)), "b": f32(0.5 * np.random.standard_normal((M, 1))), "offs": striped(np.stack([np.random.permutation(S)[:N] for _ in range(8)]))}


def reference(tab, x0, w, b, offs):
    idx = np.stack([g.T.reshape(-1) for g in np.split(offs, 8)])
    m = f64(x0)
    for d in range(D):
        m = np.maximum(m, look(tab, idx[:, d * V:(d + 1) * V]))
    x = m + np.log(np.exp(f64(x0) - m) + sum(np.exp(look(tab, idx[:, d * V:(d + 1) * V]) - m) for d in range(D)))
    return np.maximum(f64(w).T @ x + f64(b), 0.0)

@@ -1,0 +1,96 @@
+import concourse.mybir as mybir
+from concourse.masks import make_identity
+
+F32, BF16, U16 = mybir.dt.float32, mybir.dt.bfloat16, mybir.dt.uint16
+ALU = mybir.AluOpType
+ACT = mybir.ActivationFunctionType
+
+P = 128
+V = 1024
+S = 2048
+N = 2 * V
+C = 512
+CHUNKS = V // C
+H = 256
+PER = 16
+
+FLOPS = 2 * P * P * V
+
+
+def entries(offsets, d, c):
+    first = (d * V + c * C) // PER
+    return offsets[:, first : first + C // PER]
+
+
+def tile_lookup_lse_relu_kernel(tc, tab, x0, w, b, offs, out):
+    nc = tc.nc
+    with (
+        tc.tile_pool(name="held", bufs=1) as held,
+        tc.psum_pool(name="psum", bufs=1) as psum,
+        tc.psum_pool(name="products", bufs=4) as products,
+    ):
+        offsets = held.tile([P, N // PER], U16, name="offsets")
+        table = held.tile([P, S], F32, name="table")
+        node = held.tile([P, V], F32, name="node")
+        weights = held.tile([P, P], BF16, name="weights")
+        bias = held.tile([P, 1], F32, name="bias")
+        nc.sync.dma_start(offsets[:], offs)
+        nc.sync.dma_start(table[:], tab)
+        for c in range(CHUNKS):
+            nc.sync.dma_start(node[:, c * C : (c + 1) * C], x0[:, c * C : (c + 1) * C])
+        nc.sync.dma_start(weights[:], w)
+        nc.sync.dma_start(bias[:], b)
+
+        plus = held.tile([P, P], F32, name="plus")
+        minus = held.tile([P, P], F32, name="minus")
+        make_identity(nc, plus[:])
+        nc.gpsimd.tensor_scalar(minus[:], plus[:], -1.0, 0.0, ALU.mult, ALU.add)
+
+        m0 = held.tile([P, V], F32, name="m0")
+        h = held.tile([P, V], F32, name="h")
+        d0 = held.tile([P, V], F32, name="d0")
+        d1 = held.tile([P, V], F32, name="d1")
+        e0 = held.tile([P, V], F32, name="e0")
+        e1 = held.tile([P, V], F32, name="e1")
+        ex = held.tile([P, V], F32, name="ex")
+        s0 = held.tile([P, V], F32, name="s0")
+        s1 = held.tile([P, V], F32, name="s1")
+        log_s = held.tile([P, V], F32, name="log_s")
+        x = held.tile([P, V], BF16, name="x")
+        result = held.tile([P, V], F32, name="result")
+        dx_first = psum.tile([P, C], F32, name="dx_first")
+        dx_last = held.tile([P, C], F32, name="dx_last")
+        chunks = [slice(c * C, (c + 1) * C) for c in range(CHUNKS)]
+
+        for c, cols in enumerate(chunks):
+            nc.vector.tensor_tensor(m0[:, cols], table[:].indirect(entries(offsets, 0, c)), node[:, cols], ALU.max)
+        for c, cols in enumerate(chunks):
+            nc.vector.tensor_tensor(h[:, cols], table[:].indirect(entries(offsets, 1, c)), m0[:, cols], ALU.max)
+
+        nc.tensor.matmul(dx_first[:], plus[:], node[:, chunks[0]], start=True, stop=False)
+        nc.tensor.matmul(dx_first[:], minus[:], h[:, chunks[0]], start=False, stop=True)
+        nc.scalar.activation(ex[:, chunks[0]], dx_first[:], ACT.Exp)
+        nc.vector.tensor_tensor(dx_last[:], node[:, chunks[1]], h[:, chunks[1]], ALU.subtract)
+        nc.scalar.activation(ex[:, chunks[1]], dx_last[:], ACT.Exp)
+
+        for c, cols in enumerate(chunks):
+            nc.vector.tensor_tensor(d0[:, cols], table[:].indirect(entries(offsets, 0, c)), h[:, cols], ALU.subtract)
+            nc.scalar.activation(e0[:, cols], d0[:, cols], ACT.Exp)
+        for c, cols in enumerate(chunks):
+            nc.vector.tensor_tensor(d1[:, cols], table[:].indirect(entries(offsets, 1, c)), h[:, cols], ALU.subtract)
+            nc.scalar.activation(e1[:, cols], d1[:, cols], ACT.Exp)
+
+        for cols in chunks:
+            nc.vector.tensor_tensor(s0[:, cols], ex[:, cols], e0[:, cols], ALU.add)
+        nc.vector.tensor_tensor(s1[:], s0[:], e1[:], ALU.add)
+        for i in range(V // H):
+            cols = slice(i * H, (i + 1) * H)
+            nc.scalar.activation(log_s[:, cols], s1[:, cols], ACT.Ln)
+            nc.vector.tensor_tensor(x[:, cols], h[:, cols], log_s[:, cols], ALU.add)
+            product = products.tile([P, H], F32, name="product")
+            nc.tensor.matmul(product[:], weights[:], x[:, cols], start=True, stop=True)
+            if i % 2 == 0:
+                nc.scalar.activation(result[:, cols], product[:], ACT.Relu, bias=bias[:, 0:1])
+            else:
+                nc.vector.tensor_scalar(result[:, cols], product[:], bias[:, 0:1], 0.0, ALU.add, ALU.max)
+            nc.sync.dma_start(out[:, cols], result[:, cols])

@@ -10,16 +10,14 @@ V = 1024
 S = 2048
 N = 2 * V
 C = 512
-CHUNKS = V // C
-H = 256
 PER = 16
 
 FLOPS = 2 * P * P * V
+H = 256
 
 
-def entries(offsets, d, c):
-    first = (d * V + c * C) // PER
-    return offsets[:, first : first + C // PER]
+def entries(offsets, d, cols):
+    return offsets[:, (d * V + cols.start) // PER : (d * V + cols.stop) // PER]
 
 
 def tile_lookup_lse_relu_kernel(tc, tab, x0, w, b, offs, out):
@@ -29,68 +27,86 @@ def tile_lookup_lse_relu_kernel(tc, tab, x0, w, b, offs, out):
         tc.psum_pool(name="psum", bufs=1) as psum,
         tc.psum_pool(name="products", bufs=4) as products,
     ):
+        first, last = slice(0, C), slice(C, V)
+        chunks = [first, last]
+
         offsets = held.tile([P, N // PER], U16, name="offsets")
         table = held.tile([P, S], F32, name="table")
         node = held.tile([P, V], F32, name="node")
         weights = held.tile([P, P], BF16, name="weights")
         bias = held.tile([P, 1], F32, name="bias")
         nc.sync.dma_start(offsets[:], offs)
+        nc.sync.dma_start(node[:, first], x0[:, first])
         nc.sync.dma_start(table[:], tab)
-        for c in range(CHUNKS):
-            nc.sync.dma_start(node[:, c * C : (c + 1) * C], x0[:, c * C : (c + 1) * C])
+        nc.sync.dma_start(node[:, last], x0[:, last])
         nc.sync.dma_start(weights[:], w)
         nc.sync.dma_start(bias[:], b)
 
-        plus = held.tile([P, P], F32, name="plus")
-        minus = held.tile([P, P], F32, name="minus")
-        make_identity(nc, plus[:])
-        nc.gpsimd.tensor_scalar(minus[:], plus[:], -1.0, 0.0, ALU.mult, ALU.add)
+        identity = held.tile([P, P], F32, name="identity")
+        make_identity(nc, identity[:])
+
+        def add_transposed(bank, source, start, stop):
+            for k in range(C // P):
+                block = slice(k * P, (k + 1) * P)
+                nc.tensor.matmul(bank[:, block], source[:, block], identity[:], is_transpose=True,
+                                 start=start and k == 0, stop=stop and k == C // P - 1)
 
         m0 = held.tile([P, V], F32, name="m0")
         h = held.tile([P, V], F32, name="h")
         d0 = held.tile([P, V], F32, name="d0")
         d1 = held.tile([P, V], F32, name="d1")
-        e0 = held.tile([P, V], F32, name="e0")
-        e1 = held.tile([P, V], F32, name="e1")
-        ex = held.tile([P, V], F32, name="ex")
+        negated = held.tile([P, V], F32, name="negated")
+        ex_t = held.tile([P, V], F32, name="ex_t")
         s0 = held.tile([P, V], F32, name="s0")
-        s1 = held.tile([P, V], F32, name="s1")
-        log_s = held.tile([P, V], F32, name="log_s")
+        s_last = held.tile([P, C], F32, name="s_last")
+        logs = held.tile([P, V], F32, name="logs")
         x = held.tile([P, V], BF16, name="x")
         result = held.tile([P, V], F32, name="result")
-        dx_first = psum.tile([P, C], F32, name="dx_first")
-        dx_last = held.tile([P, C], F32, name="dx_last")
-        chunks = [slice(c * C, (c + 1) * C) for c in range(CHUNKS)]
-
-        for c, cols in enumerate(chunks):
-            nc.vector.tensor_tensor(m0[:, cols], table[:].indirect(entries(offsets, 0, c)), node[:, cols], ALU.max)
-        for c, cols in enumerate(chunks):
-            nc.vector.tensor_tensor(h[:, cols], table[:].indirect(entries(offsets, 1, c)), m0[:, cols], ALU.max)
-
-        nc.tensor.matmul(dx_first[:], plus[:], node[:, chunks[0]], start=True, stop=False)
-        nc.tensor.matmul(dx_first[:], minus[:], h[:, chunks[0]], start=False, stop=True)
-        nc.scalar.activation(ex[:, chunks[0]], dx_first[:], ACT.Exp)
-        nc.vector.tensor_tensor(dx_last[:], node[:, chunks[1]], h[:, chunks[1]], ALU.subtract)
-        nc.scalar.activation(ex[:, chunks[1]], dx_last[:], ACT.Exp)
-
-        for c, cols in enumerate(chunks):
-            nc.vector.tensor_tensor(d0[:, cols], table[:].indirect(entries(offsets, 0, c)), h[:, cols], ALU.subtract)
-            nc.scalar.activation(e0[:, cols], d0[:, cols], ACT.Exp)
-        for c, cols in enumerate(chunks):
-            nc.vector.tensor_tensor(d1[:, cols], table[:].indirect(entries(offsets, 1, c)), h[:, cols], ALU.subtract)
-            nc.scalar.activation(e1[:, cols], d1[:, cols], ACT.Exp)
+        dx = [psum.tile([P, C], F32, name=f"dx{c}") for c in range(len(chunks))]
+        ex = [psum.tile([P, C], F32, name=f"ex{c}") for c in range(len(chunks))]
 
         for cols in chunks:
-            nc.vector.tensor_tensor(s0[:, cols], ex[:, cols], e0[:, cols], ALU.add)
-        nc.vector.tensor_tensor(s1[:], s0[:], e1[:], ALU.add)
-        for i in range(V // H):
-            cols = slice(i * H, (i + 1) * H)
-            nc.scalar.activation(log_s[:, cols], s1[:, cols], ACT.Ln)
-            nc.vector.tensor_tensor(x[:, cols], h[:, cols], log_s[:, cols], ALU.add)
+            nc.vector.tensor_tensor(m0[:, cols], table[:].indirect(entries(offsets, 0, cols)), node[:, cols], ALU.max)
+        for cols in chunks:
+            nc.vector.tensor_tensor(h[:, cols], table[:].indirect(entries(offsets, 1, cols)), m0[:, cols], ALU.max)
+        for cols in chunks:
+            nc.vector.tensor_tensor(d0[:, cols], table[:].indirect(entries(offsets, 0, cols)), h[:, cols], ALU.subtract)
+        for cols in chunks:
+            nc.vector.tensor_tensor(d1[:, cols], table[:].indirect(entries(offsets, 1, cols)), h[:, cols], ALU.subtract)
+
+        for cols in chunks:
+            nc.scalar.mul(negated[:, cols], node[:, cols], -1.0)
+        for c, cols in enumerate(chunks):
+            add_transposed(dx[c], negated[:, cols], start=True, stop=False)
+        for c, cols in enumerate(chunks):
+            add_transposed(dx[c], h[:, cols], start=False, stop=True)
+            nc.scalar.activation(ex_t[:, cols], dx[c][:], ACT.Exp, scale=-1.0)
+            add_transposed(ex[c], ex_t[:, cols], start=True, stop=True)
+
+        e0, e1 = ex_t, d0
+        for cols in chunks:
+            nc.scalar.activation(e0[:, cols], d0[:, cols], ACT.Exp)
+        for cols in chunks:
+            nc.scalar.activation(e1[:, cols], d1[:, cols], ACT.Exp)
+
+        for c in reversed(range(len(chunks))):
+            nc.vector.tensor_tensor(s0[:, chunks[c]], ex[c][:], e0[:, chunks[c]], ALU.add)
+        nc.vector.tensor_tensor(s_last[:], s0[:, last], e1[:, last], ALU.add)
+        s_first = s0[:, last]
+        nc.vector.tensor_tensor(s_first, s0[:, first], e1[:, first], ALU.add)
+
+        pieces = []
+        for cols, sums in [(last, s_last[:]), (first, s_first)]:
+            for start in range(0, C, H):
+                piece = slice(cols.start + start, cols.start + start + H)
+                nc.scalar.activation(logs[:, piece], sums[:, start : start + H], ACT.Ln)
+                nc.vector.tensor_tensor(x[:, piece], h[:, piece], logs[:, piece], ALU.add)
+                pieces.append(piece)
+        for piece in pieces:
             product = products.tile([P, H], F32, name="product")
-            nc.tensor.matmul(product[:], weights[:], x[:, cols], start=True, stop=True)
-            if i % 2 == 0:
-                nc.scalar.activation(result[:, cols], product[:], ACT.Relu, bias=bias[:, 0:1])
+            nc.tensor.matmul(product[:], weights[:], x[:, piece], start=True, stop=True)
+            if piece is not pieces[-1]:
+                nc.scalar.activation(result[:, piece], product[:], ACT.Relu, bias=bias[:, 0:1])
             else:
-                nc.vector.tensor_scalar(result[:, cols], product[:], bias[:, 0:1], 0.0, ALU.add, ALU.max)
-            nc.sync.dma_start(out[:, cols], result[:, cols])
+                nc.vector.tensor_scalar(result[:, piece], product[:], bias[:, 0:1], 0.0, ALU.add, ALU.max)
+            nc.sync.dma_start(out[:, piece], result[:, piece])

@@ -13,7 +13,7 @@ C = 512
 PER = 16
 
 FLOPS = 2 * P * P * V
-H = 256
+WIDTHS = [[256, 256], [256, 128, 128]]
 
 
 def entries(offsets, d, cols):
@@ -57,9 +57,9 @@ def tile_lookup_lse_relu_kernel(tc, tab, x0, w, b, offs, out):
         d1 = held.tile([P, V], F32, name="d1")
         negated = held.tile([P, V], F32, name="negated")
         ex_t = held.tile([P, V], F32, name="ex_t")
-        s0 = held.tile([P, V], F32, name="s0")
+        s0 = held.tile([P, C], F32, name="s0")
         s_last = held.tile([P, C], F32, name="s_last")
-        logs = held.tile([P, V], F32, name="logs")
+        logs_last = held.tile([P, C], F32, name="logs_last")
         x = held.tile([P, V], BF16, name="x")
         result = held.tile([P, V], F32, name="result")
         dx = [psum.tile([P, C], F32, name=f"dx{c}") for c in range(len(chunks))]
@@ -81,31 +81,33 @@ def tile_lookup_lse_relu_kernel(tc, tab, x0, w, b, offs, out):
         for c, cols in enumerate(chunks):
             add_transposed(dx[c], h[:, cols], start=False, stop=True)
             nc.scalar.activation(ex_t[:, cols], dx[c][:], ACT.Exp, scale=-1.0)
-            add_transposed(ex[c], ex_t[:, cols], start=True, stop=True)
+            add_transposed(ex[c], ex_t[:, cols], start=True, stop=cols is last)
 
-        e0, e1 = ex_t, d0
+        e0 = ex_t
+        e1_first, e1_last = d0[:, last], d1[:, first]
         for cols in chunks:
             nc.scalar.activation(e0[:, cols], d0[:, cols], ACT.Exp)
-        for cols in chunks:
-            nc.scalar.activation(e1[:, cols], d1[:, cols], ACT.Exp)
+        nc.scalar.activation(e1_first, d1[:, first], ACT.Exp)
+        nc.scalar.activation(e1_last, d1[:, last], ACT.Exp)
 
-        for c in reversed(range(len(chunks))):
-            nc.vector.tensor_tensor(s0[:, chunks[c]], ex[c][:], e0[:, chunks[c]], ALU.add)
-        nc.vector.tensor_tensor(s_last[:], s0[:, last], e1[:, last], ALU.add)
-        s_first = s0[:, last]
-        nc.vector.tensor_tensor(s_first, s0[:, first], e1[:, first], ALU.add)
+        nc.tensor.matmul(ex[0][:], identity[:], e0[:, first], start=False, stop=False)
+        nc.tensor.matmul(ex[0][:], identity[:], e1_first, start=False, stop=True)
+        nc.vector.tensor_tensor(s0[:], ex[1][:], e0[:, last], ALU.add)
+        nc.vector.tensor_tensor(s_last[:], s0[:], e1_last, ALU.add)
 
         pieces = []
-        for cols, sums in [(last, s_last[:]), (first, s_first)]:
-            for start in range(0, C, H):
-                piece = slice(cols.start + start, cols.start + start + H)
-                nc.scalar.activation(logs[:, piece], sums[:, start : start + H], ACT.Ln)
-                nc.vector.tensor_tensor(x[:, piece], h[:, piece], logs[:, piece], ALU.add)
+        for cols, sums, logs, widths in zip([last, first], [s_last, ex[0]], [logs_last, s_last], WIDTHS):
+            start = 0
+            for width in widths:
+                piece = slice(cols.start + start, cols.start + start + width)
+                nc.scalar.activation(logs[:, start : start + width], sums[:, start : start + width], ACT.Ln)
+                nc.vector.tensor_tensor(x[:, piece], h[:, piece], logs[:, start : start + width], ALU.add)
                 pieces.append(piece)
-        for piece in pieces:
-            product = products.tile([P, H], F32, name="product")
+                start += width
+        for i, piece in enumerate(pieces):
+            product = products.tile([P, piece.stop - piece.start], F32, name="product")
             nc.tensor.matmul(product[:], weights[:], x[:, piece], start=True, stop=True)
-            if piece is not pieces[-1]:
+            if i < 2 or i % 2 == 1:
                 nc.scalar.activation(result[:, piece], product[:], ACT.Relu, bias=bias[:, 0:1])
             else:
                 nc.vector.tensor_scalar(result[:, piece], product[:], bias[:, 0:1], 0.0, ALU.add, ALU.max)

@@ -13,7 +13,7 @@ C = 512
 PER = 16
 
 FLOPS = 2 * P * P * V
-WIDTHS = [[256, 256], [256, 128, 128]]
+WIDTHS = [[128, 192, 192], [192, 192, 128]]
 
 
 def entries(offsets, d, cols):
@@ -25,7 +25,7 @@ def tile_lookup_lse_relu_kernel(tc, tab, x0, w, b, offs, out):
     with (
         tc.tile_pool(name="held", bufs=1) as held,
         tc.psum_pool(name="psum", bufs=1) as psum,
-        tc.psum_pool(name="products", bufs=4) as products,
+        tc.psum_pool(name="ring", bufs=6) as ring,
     ):
         first, last = slice(0, C), slice(C, V)
         chunks = [first, last]
@@ -35,9 +35,9 @@ def tile_lookup_lse_relu_kernel(tc, tab, x0, w, b, offs, out):
         node = held.tile([P, V], F32, name="node")
         weights = held.tile([P, P], BF16, name="weights")
         bias = held.tile([P, 1], F32, name="bias")
-        nc.sync.dma_start(offsets[:], offs)
-        nc.sync.dma_start(node[:, first], x0[:, first])
         nc.sync.dma_start(table[:], tab)
+        nc.sync.dma_start(node[:, first], x0[:, first])
+        nc.sync.dma_start(offsets[:], offs)
         nc.sync.dma_start(node[:, last], x0[:, last])
         nc.sync.dma_start(weights[:], w)
         nc.sync.dma_start(bias[:], b)
@@ -57,12 +57,11 @@ def tile_lookup_lse_relu_kernel(tc, tab, x0, w, b, offs, out):
         d1 = held.tile([P, V], F32, name="d1")
         negated = held.tile([P, V], F32, name="negated")
         ex_t = held.tile([P, V], F32, name="ex_t")
-        s0 = held.tile([P, C], F32, name="s0")
         s_last = held.tile([P, C], F32, name="s_last")
         logs_last = held.tile([P, C], F32, name="logs_last")
         x = held.tile([P, V], BF16, name="x")
         result = held.tile([P, V], F32, name="result")
-        dx = [psum.tile([P, C], F32, name=f"dx{c}") for c in range(len(chunks))]
+        dx = [ring.tile([P, C], F32, name=f"dx{c}", tag="bank") for c in range(len(chunks))]
         ex = [psum.tile([P, C], F32, name=f"ex{c}") for c in range(len(chunks))]
 
         for cols in chunks:
@@ -81,7 +80,7 @@ def tile_lookup_lse_relu_kernel(tc, tab, x0, w, b, offs, out):
         for c, cols in enumerate(chunks):
             add_transposed(dx[c], h[:, cols], start=False, stop=True)
             nc.scalar.activation(ex_t[:, cols], dx[c][:], ACT.Exp, scale=-1.0)
-            add_transposed(ex[c], ex_t[:, cols], start=True, stop=cols is last)
+            add_transposed(ex[c], ex_t[:, cols], start=True, stop=False)
 
         e0 = ex_t
         e1_first, e1_last = d0[:, last], d1[:, first]
@@ -91,9 +90,9 @@ def tile_lookup_lse_relu_kernel(tc, tab, x0, w, b, offs, out):
         nc.scalar.activation(e1_last, d1[:, last], ACT.Exp)
 
         nc.tensor.matmul(ex[0][:], identity[:], e0[:, first], start=False, stop=False)
+        nc.tensor.matmul(ex[1][:], identity[:], e0[:, last], start=False, stop=True)
         nc.tensor.matmul(ex[0][:], identity[:], e1_first, start=False, stop=True)
-        nc.vector.tensor_tensor(s0[:], ex[1][:], e0[:, last], ALU.add)
-        nc.vector.tensor_tensor(s_last[:], s0[:], e1_last, ALU.add)
+        nc.vector.tensor_tensor(s_last[:], ex[1][:], e1_last, ALU.add)
 
         pieces = []
         for cols, sums, logs, widths in zip([last, first], [s_last, ex[0]], [logs_last, s_last], WIDTHS):
@@ -105,9 +104,9 @@ def tile_lookup_lse_relu_kernel(tc, tab, x0, w, b, offs, out):
                 pieces.append(piece)
                 start += width
         for i, piece in enumerate(pieces):
-            product = products.tile([P, piece.stop - piece.start], F32, name="product")
+            product = ring.tile([P, piece.stop - piece.start], F32, name="product", tag="bank")
             nc.tensor.matmul(product[:], weights[:], x[:, piece], start=True, stop=True)
-            if i < 2 or i % 2 == 1:
+            if i < 3 or i % 2 == 0:
                 nc.scalar.activation(result[:, piece], product[:], ACT.Relu, bias=bias[:, 0:1])
             else:
                 nc.vector.tensor_scalar(result[:, piece], product[:], bias[:, 0:1], 0.0, ALU.add, ALU.max)

@@ -13,7 +13,7 @@ C = 512
 PER = 16
 
 FLOPS = 2 * P * P * V
-WIDTHS = [[128, 192, 192], [192, 192, 128]]
+W = 128
 
 
 def entries(offsets, d, cols):
@@ -95,19 +95,19 @@ def tile_lookup_lse_relu_kernel(tc, tab, x0, w, b, offs, out):
         nc.vector.tensor_tensor(s_last[:], ex[1][:], e1_last, ALU.add)
 
         pieces = []
-        for cols, sums, logs, widths in zip([last, first], [s_last, ex[0]], [logs_last, s_last], WIDTHS):
-            start = 0
-            for width in widths:
-                piece = slice(cols.start + start, cols.start + start + width)
-                nc.scalar.activation(logs[:, start : start + width], sums[:, start : start + width], ACT.Ln)
-                nc.vector.tensor_tensor(x[:, piece], h[:, piece], logs[:, start : start + width], ALU.add)
+        for cols, sums, logs in zip([last, first], [s_last, ex[0]], [logs_last, s_last]):
+            for start in range(0, C, W):
+                piece = slice(cols.start + start, cols.start + start + W)
+                nc.scalar.activation(logs[:, start : start + W], sums[:, start : start + W], ACT.Ln)
+                nc.vector.tensor_tensor(x[:, piece], h[:, piece], logs[:, start : start + W], ALU.add)
                 pieces.append(piece)
-                start += width
         for i, piece in enumerate(pieces):
-            product = ring.tile([P, piece.stop - piece.start], F32, name="product", tag="bank")
+            product = ring.tile([P, W], F32, name="product", tag="bank")
             nc.tensor.matmul(product[:], weights[:], x[:, piece], start=True, stop=True)
             if i < 3 or i % 2 == 0:
                 nc.scalar.activation(result[:, piece], product[:], ACT.Relu, bias=bias[:, 0:1])
             else:
                 nc.vector.tensor_scalar(result[:, piece], product[:], bias[:, 0:1], 0.0, ALU.add, ALU.max)
-            nc.sync.dma_start(out[:, piece], result[:, piece])
+            if i % 2 == 1:
+                pair = slice(piece.start - W, piece.stop)
+                nc.sync.dma_start(out[:, pair], result[:, pair])

@@ -24,8 +24,7 @@ def tile_lookup_lse_relu_kernel(tc, tab, x0, w, b, offs, out):
     nc = tc.nc
     with (
         tc.tile_pool(name="held", bufs=1) as held,
-        tc.psum_pool(name="psum", bufs=1) as psum,
-        tc.psum_pool(name="ring", bufs=6) as ring,
+        tc.psum_pool(name="ring", bufs=8) as ring,
     ):
         first, last = slice(0, C), slice(C, V)
         chunks = [first, last]
@@ -46,10 +45,11 @@ def tile_lookup_lse_relu_kernel(tc, tab, x0, w, b, offs, out):
         make_identity(nc, identity[:])
 
         def add_transposed(bank, source, start, stop):
-            for k in range(C // P):
+            blocks = source.shape[1] // P
+            for k in range(blocks):
                 block = slice(k * P, (k + 1) * P)
                 nc.tensor.matmul(bank[:, block], source[:, block], identity[:], is_transpose=True,
-                                 start=start and k == 0, stop=stop and k == C // P - 1)
+                                 start=start and k == 0, stop=stop and k == blocks - 1)
 
         m0 = held.tile([P, V], F32, name="m0")
         h = held.tile([P, V], F32, name="h")
@@ -57,12 +57,14 @@ def tile_lookup_lse_relu_kernel(tc, tab, x0, w, b, offs, out):
         d1 = held.tile([P, V], F32, name="d1")
         negated = held.tile([P, V], F32, name="negated")
         ex_t = held.tile([P, V], F32, name="ex_t")
-        s_last = held.tile([P, C], F32, name="s_last")
-        logs_last = held.tile([P, C], F32, name="logs_last")
+        s_early = held.tile([P, C // 2], F32, name="s_early")
+        logs = held.tile([P, V], F32, name="logs")
         x = held.tile([P, V], BF16, name="x")
         result = held.tile([P, V], F32, name="result")
         dx = [ring.tile([P, C], F32, name=f"dx{c}", tag="bank") for c in range(len(chunks))]
-        ex = [psum.tile([P, C], F32, name=f"ex{c}") for c in range(len(chunks))]
+        early, late = slice(C, C + C // 2), slice(C + C // 2, V)
+        parts = [first, early, late]
+        ex = [ring.tile([P, cols.stop - cols.start], F32, name=f"ex{c}", tag="bank") for c, cols in enumerate(parts)]
 
         for cols in chunks:
             nc.vector.tensor_tensor(m0[:, cols], table[:].indirect(entries(offsets, 0, cols)), node[:, cols], ALU.max)
@@ -80,7 +82,8 @@ def tile_lookup_lse_relu_kernel(tc, tab, x0, w, b, offs, out):
         for c, cols in enumerate(chunks):
             add_transposed(dx[c], h[:, cols], start=False, stop=True)
             nc.scalar.activation(ex_t[:, cols], dx[c][:], ACT.Exp, scale=-1.0)
-            add_transposed(ex[c], ex_t[:, cols], start=True, stop=False)
+        for bank, cols in zip(ex, parts):
+            add_transposed(bank, ex_t[:, cols], start=True, stop=False)
 
         e0 = ex_t
         e1_first, e1_last = d0[:, last], d1[:, first]
@@ -89,17 +92,18 @@ def tile_lookup_lse_relu_kernel(tc, tab, x0, w, b, offs, out):
         nc.scalar.activation(e1_first, d1[:, first], ACT.Exp)
         nc.scalar.activation(e1_last, d1[:, last], ACT.Exp)
 
-        nc.tensor.matmul(ex[0][:], identity[:], e0[:, first], start=False, stop=False)
-        nc.tensor.matmul(ex[1][:], identity[:], e0[:, last], start=False, stop=True)
+        for bank, cols in zip(ex, parts):
+            nc.tensor.matmul(bank[:], identity[:], e0[:, cols], start=False, stop=cols == early)
         nc.tensor.matmul(ex[0][:], identity[:], e1_first, start=False, stop=True)
-        nc.vector.tensor_tensor(s_last[:], ex[1][:], e1_last, ALU.add)
+        nc.tensor.matmul(ex[2][:], identity[:], e1_last[:, C // 2 :], start=False, stop=True)
+        nc.vector.tensor_tensor(s_early[:], ex[1][:], e1_last[:, : C // 2], ALU.add)
 
         pieces = []
-        for cols, sums, logs in zip([last, first], [s_last, ex[0]], [logs_last, s_last]):
-            for start in range(0, C, W):
+        for cols, sums in zip([early, first, late], [s_early, ex[0], ex[2]]):
+            for start in range(0, cols.stop - cols.start, W):
                 piece = slice(cols.start + start, cols.start + start + W)
-                nc.scalar.activation(logs[:, start : start + W], sums[:, start : start + W], ACT.Ln)
-                nc.vector.tensor_tensor(x[:, piece], h[:, piece], logs[:, start : start + W], ALU.add)
+                nc.scalar.activation(logs[:, piece], sums[:, start : start + W], ACT.Ln)
+                nc.vector.tensor_tensor(x[:, piece], h[:, piece], logs[:, piece], ALU.add)
                 pieces.append(piece)
         for i, piece in enumerate(pieces):
             product = ring.tile([P, W], F32, name="product", tag="bank")

@@ -34,7 +34,8 @@ def tile_lookup_lse_relu_kernel(tc, tab, x0, w, b, offs, out):
         node = held.tile([P, V], F32, name="node")
         weights = held.tile([P, P], BF16, name="weights")
         bias = held.tile([P, 1], F32, name="bias")
-        nc.sync.dma_start(table[:], tab)
+        nc.sync.dma_start(table[:, : S // 2], tab[:, : S // 2])
+        nc.scalar.dma_start(table[:, S // 2 :], tab[:, S // 2 :])
         nc.sync.dma_start(node[:, first], x0[:, first])
         nc.sync.dma_start(offsets[:], offs)
         nc.sync.dma_start(node[:, last], x0[:, last])
@@ -85,15 +86,16 @@ def tile_lookup_lse_relu_kernel(tc, tab, x0, w, b, offs, out):
         for bank, cols in zip(ex, parts):
             add_transposed(bank, ex_t[:, cols], start=True, stop=False)
 
-        e0 = ex_t
+        e0_first, e0_last = ex_t[:, first], d0[:, first]
         e1_first, e1_last = d0[:, last], d1[:, first]
-        for cols in chunks:
-            nc.scalar.activation(e0[:, cols], d0[:, cols], ACT.Exp)
+        nc.scalar.activation(e0_first, d0[:, first], ACT.Exp)
+        nc.scalar.activation(e0_last, d0[:, last], ACT.Exp)
         nc.scalar.activation(e1_first, d1[:, first], ACT.Exp)
         nc.scalar.activation(e1_last, d1[:, last], ACT.Exp)
 
-        for bank, cols in zip(ex, parts):
-            nc.tensor.matmul(bank[:], identity[:], e0[:, cols], start=False, stop=cols == early)
+        nc.tensor.matmul(ex[0][:], identity[:], e0_first, start=False, stop=False)
+        nc.tensor.matmul(ex[1][:], identity[:], e0_last[:, : C // 2], start=False, stop=True)
+        nc.tensor.matmul(ex[2][:], identity[:], e0_last[:, C // 2 :], start=False, stop=False)
         nc.tensor.matmul(ex[0][:], identity[:], e1_first, start=False, stop=True)
         nc.tensor.matmul(ex[2][:], identity[:], e1_last[:, C // 2 :], start=False, stop=True)
         nc.vector.tensor_tensor(s_early[:], ex[1][:], e1_last[:, : C // 2], ALU.add)

@@ -12,6 +12,8 @@ N = 2 * V
 C = 512
 PER = 16
 
+SPLIT = (S - C) // 2
+
 FLOPS = 2 * P * P * V
 W = 128
 
@@ -34,10 +36,10 @@ def tile_lookup_lse_relu_kernel(tc, tab, x0, w, b, offs, out):
         node = held.tile([P, V], F32, name="node")
         weights = held.tile([P, P], BF16, name="weights")
         bias = held.tile([P, 1], F32, name="bias")
-        nc.sync.dma_start(table[:, : S // 2], tab[:, : S // 2])
-        nc.scalar.dma_start(table[:, S // 2 :], tab[:, S // 2 :])
+        nc.scalar.dma_start(table[:, SPLIT:], tab[:, SPLIT:])
         nc.sync.dma_start(node[:, first], x0[:, first])
         nc.sync.dma_start(offsets[:], offs)
+        nc.sync.dma_start(table[:, :SPLIT], tab[:, :SPLIT])
         nc.sync.dma_start(node[:, last], x0[:, last])
         nc.sync.dma_start(weights[:], w)
         nc.sync.dma_start(bias[:], b)

@@ -55,9 +55,16 @@ def tile_lookup_lse_relu_kernel(tc, tab, x0, w, b, offs, out):
                                  start=start and k == 0, stop=stop and k == blocks - 1)
 
         m0 = held.tile([P, V], F32, name="m0")
-        h = held.tile([P, V], F32, name="h")
-        d0 = held.tile([P, V], F32, name="d0")
-        d1 = held.tile([P, V], F32, name="d1")
+        h_swapped = held.tile([P, V], F32, name="h_swapped")
+        front = held.tile([P, V], F32, name="front")
+        middle = held.tile([P, V], F32, name="middle")
+        d1_last = held.tile([P, C], F32, name="d1_last")
+        d0_first, d0_last, d1_first = front[:, C // 2 : C // 2 + C], middle[:, :C], middle[:, C:]
+
+        def h(cols):
+            start = (cols.start + C) % V
+            return h_swapped[:, start : start + cols.stop - cols.start]
+
         negated = held.tile([P, V], F32, name="negated")
         ex_t = held.tile([P, V], F32, name="ex_t")
         s_early = held.tile([P, C // 2], F32, name="s_early")
@@ -72,28 +79,30 @@ def tile_lookup_lse_relu_kernel(tc, tab, x0, w, b, offs, out):
         for cols in chunks:
             nc.vector.tensor_tensor(m0[:, cols], table[:].indirect(entries(offsets, 0, cols)), node[:, cols], ALU.max)
         for cols in chunks:
-            nc.vector.tensor_tensor(h[:, cols], table[:].indirect(entries(offsets, 1, cols)), m0[:, cols], ALU.max)
-        for cols in chunks:
-            nc.vector.tensor_tensor(d0[:, cols], table[:].indirect(entries(offsets, 0, cols)), h[:, cols], ALU.subtract)
-        for cols in chunks:
-            nc.vector.tensor_tensor(d1[:, cols], table[:].indirect(entries(offsets, 1, cols)), h[:, cols], ALU.subtract)
+            nc.vector.tensor_tensor(h(cols), table[:].indirect(entries(offsets, 1, cols)), m0[:, cols], ALU.max)
+        for diffs, part, maxima in [
+            (d0_first, slice(0, C), h(first)),
+            (middle[:], slice(C, N - C), h_swapped[:]),
+            (d1_last[:], slice(N - C, N), h(last)),
+        ]:
+            nc.vector.tensor_tensor(diffs, table[:].indirect(entries(offsets, 0, part)), maxima, ALU.subtract)
 
         for cols in chunks:
             nc.scalar.mul(negated[:, cols], node[:, cols], -1.0)
         for c, cols in enumerate(chunks):
             add_transposed(dx[c], negated[:, cols], start=True, stop=False)
         for c, cols in enumerate(chunks):
-            add_transposed(dx[c], h[:, cols], start=False, stop=True)
+            add_transposed(dx[c], h(cols), start=False, stop=True)
             nc.scalar.activation(ex_t[:, cols], dx[c][:], ACT.Exp, scale=-1.0)
         for bank, cols in zip(ex, parts):
             add_transposed(bank, ex_t[:, cols], start=True, stop=False)
 
-        e0_first, e0_last = ex_t[:, first], d0[:, first]
-        e1_first, e1_last = d0[:, last], d1[:, first]
-        nc.scalar.activation(e0_first, d0[:, first], ACT.Exp)
-        nc.scalar.activation(e0_last, d0[:, last], ACT.Exp)
-        nc.scalar.activation(e1_first, d1[:, first], ACT.Exp)
-        nc.scalar.activation(e1_last, d1[:, last], ACT.Exp)
+        e0_first, e0_last = ex_t[:, first], front[:, :C]
+        e1_first, e1_last = front[:, C:], d0_last
+        nc.scalar.activation(e0_first, d0_first, ACT.Exp)
+        nc.scalar.activation(e0_last, d0_last, ACT.Exp)
+        nc.scalar.activation(e1_first, d1_first, ACT.Exp)
+        nc.scalar.activation(e1_last, d1_last[:], ACT.Exp)
 
         nc.tensor.matmul(ex[0][:], identity[:], e0_first, start=False, stop=False)
         nc.tensor.matmul(ex[1][:], identity[:], e0_last[:, : C // 2], start=False, stop=True)
@@ -107,7 +116,7 @@ def tile_lookup_lse_relu_kernel(tc, tab, x0, w, b, offs, out):
             for start in range(0, cols.stop - cols.start, W):
                 piece = slice(cols.start + start, cols.start + start + W)
                 nc.scalar.activation(logs[:, piece], sums[:, start : start + W], ACT.Ln)
-                nc.vector.tensor_tensor(x[:, piece], h[:, piece], logs[:, piece], ALU.add)
+                nc.vector.tensor_tensor(x[:, piece], h(piece), logs[:, piece], ALU.add)
                 pieces.append(piece)
         for i, piece in enumerate(pieces):
             product = ring.tile([P, W], F32, name="product", tag="bank")

@@ -68,9 +68,9 @@ def tile_lookup_lse_relu_kernel(tc, tab, x0, w, b, offs, out):
         negated = held.tile([P, V], F32, name="negated")
         ex_t = held.tile([P, V], F32, name="ex_t")
         s_early = held.tile([P, C // 2], F32, name="s_early")
-        logs = held.tile([P, V], F32, name="logs")
+        logs = held.tile([P, V + W], F32, name="logs")
         x = held.tile([P, V], BF16, name="x")
-        result = held.tile([P, V], F32, name="result")
+        weights32 = held.tile([P, P], F32, name="weights32")
         dx = [ring.tile([P, C], F32, name=f"dx{c}", tag="bank") for c in range(len(chunks))]
         early, late = slice(C, C + C // 2), slice(C + C // 2, V)
         parts = [first, early, late]
@@ -111,20 +111,30 @@ def tile_lookup_lse_relu_kernel(tc, tab, x0, w, b, offs, out):
         nc.tensor.matmul(ex[2][:], identity[:], e1_last[:, C // 2 :], start=False, stop=True)
         nc.vector.tensor_tensor(s_early[:], ex[1][:], e1_last[:, : C // 2], ALU.add)
 
-        pieces = []
-        for cols, sums in zip([early, first, late], [s_early, ex[0], ex[2]]):
-            for start in range(0, cols.stop - cols.start, W):
-                piece = slice(cols.start + start, cols.start + start + W)
-                nc.scalar.activation(logs[:, piece], sums[:, start : start + W], ACT.Ln)
-                nc.vector.tensor_tensor(x[:, piece], h(piece), logs[:, piece], ALU.add)
-                pieces.append(piece)
+        parts_in_turn = [(early, s_early), (first, ex[0]), (late, ex[2])]
+        pieces = [slice(c, c + W) for cols, sums in parts_in_turn for c in range(cols.start, cols.stop, W)]
+        sums = [sums[:, c : c + W] for cols, sums in parts_in_turn for c in range(0, cols.stop - cols.start, W)]
+        exact = [0, 2, 4]
+        nc.scalar.copy(weights32[:], weights[:])
+        products = {}
+        for i in exact:
+            products[i] = ring.tile([P, W], F32, name="product", tag="bank")
+            nc.tensor.matmul(products[i][:], weights32[:], h(pieces[i]), start=True, stop=False)
+        for i in range(len(pieces)):
+            nc.scalar.activation(logs[:, i * W : (i + 1) * W], sums[i], ACT.Ln)
         for i, piece in enumerate(pieces):
-            product = ring.tile([P, W], F32, name="product", tag="bank")
-            nc.tensor.matmul(product[:], weights[:], x[:, piece], start=True, stop=True)
-            if i < 3 or i % 2 == 0:
-                nc.scalar.activation(result[:, piece], product[:], ACT.Relu, bias=bias[:, 0:1])
+            if i in exact:
+                nc.tensor.matmul(products[i][:], weights32[:], logs[:, i * W : (i + 1) * W], start=False, stop=True)
             else:
-                nc.vector.tensor_scalar(result[:, piece], product[:], bias[:, 0:1], 0.0, ALU.add, ALU.max)
+                products[i] = ring.tile([P, W], F32, name="product", tag="bank")
+                nc.vector.tensor_tensor(x[:, piece], h(piece), logs[:, i * W : (i + 1) * W], ALU.add)
+                nc.tensor.matmul(products[i][:], weights[:], x[:, piece], start=True, stop=True)
+        results = [h_swapped[:, C + W : C + 3 * W], h_swapped[:, C - W : C + W], logs[:, V - W :], m0[:, : 2 * W]]
+        for i, piece in enumerate(pieces):
+            result = results[i // 2][:, i % 2 * W : (i % 2 + 1) * W]
+            if i in (1, 3, 5, 6):
+                nc.scalar.activation(result, products[i][:], ACT.Relu, bias=bias[:, 0:1])
+            else:
+                nc.vector.tensor_scalar(result, products[i][:], bias[:, 0:1], 0.0, ALU.add, ALU.max)
             if i % 2 == 1:
-                pair = slice(piece.start - W, piece.stop)
-                nc.sync.dma_start(out[:, pair], result[:, pair])
+                nc.sync.dma_start(out[:, piece.start - W : piece.stop], results[i // 2])

@@ -67,14 +67,12 @@ def tile_lookup_lse_relu_kernel(tc, tab, x0, w, b, offs, out):
 
         negated = held.tile([P, V], F32, name="negated")
         ex_t = held.tile([P, V], F32, name="ex_t")
-        s_early = held.tile([P, C // 2], F32, name="s_early")
-        logs = held.tile([P, V + W], F32, name="logs")
+        s_last = held.tile([P, C], F32, name="s_last")
+        logs = held.tile([P, V], F32, name="logs")
+        result = held.tile([P, V], F32, name="result")
         x = held.tile([P, V], BF16, name="x")
-        weights32 = held.tile([P, P], F32, name="weights32")
         dx = [ring.tile([P, C], F32, name=f"dx{c}", tag="bank") for c in range(len(chunks))]
-        early, late = slice(C, C + C // 2), slice(C + C // 2, V)
-        parts = [first, early, late]
-        ex = [ring.tile([P, cols.stop - cols.start], F32, name=f"ex{c}", tag="bank") for c, cols in enumerate(parts)]
+        ex = [ring.tile([P, C], F32, name=f"ex{c}", tag="bank") for c in range(len(chunks))]
 
         for cols in chunks:
             nc.vector.tensor_tensor(m0[:, cols], table[:].indirect(entries(offsets, 0, cols)), node[:, cols], ALU.max)
@@ -82,7 +80,7 @@ def tile_lookup_lse_relu_kernel(tc, tab, x0, w, b, offs, out):
             nc.vector.tensor_tensor(h(cols), table[:].indirect(entries(offsets, 1, cols)), m0[:, cols], ALU.max)
         for diffs, part, maxima in [
             (d0_first, slice(0, C), h(first)),
-            (middle[:], slice(C, N - C), h_swapped[:]),
+            (middle[:], slice(C, N - C), h_swapped[:, :V]),
             (d1_last[:], slice(N - C, N), h(last)),
         ]:
             nc.vector.tensor_tensor(diffs, table[:].indirect(entries(offsets, 0, part)), maxima, ALU.subtract)
@@ -94,7 +92,7 @@ def tile_lookup_lse_relu_kernel(tc, tab, x0, w, b, offs, out):
         for c, cols in enumerate(chunks):
             add_transposed(dx[c], h(cols), start=False, stop=True)
             nc.scalar.activation(ex_t[:, cols], dx[c][:], ACT.Exp, scale=-1.0)
-        for bank, cols in zip(ex, parts):
+        for bank, cols in zip(ex, chunks):
             add_transposed(bank, ex_t[:, cols], start=True, stop=False)
 
         e0_first, e0_last = ex_t[:, first], front[:, :C]
@@ -105,36 +103,33 @@ def tile_lookup_lse_relu_kernel(tc, tab, x0, w, b, offs, out):
         nc.scalar.activation(e1_last, d1_last[:], ACT.Exp)
 
         nc.tensor.matmul(ex[0][:], identity[:], e0_first, start=False, stop=False)
-        nc.tensor.matmul(ex[1][:], identity[:], e0_last[:, : C // 2], start=False, stop=True)
-        nc.tensor.matmul(ex[2][:], identity[:], e0_last[:, C // 2 :], start=False, stop=False)
+        nc.tensor.matmul(ex[1][:], identity[:], e0_last, start=False, stop=True)
         nc.tensor.matmul(ex[0][:], identity[:], e1_first, start=False, stop=True)
-        nc.tensor.matmul(ex[2][:], identity[:], e1_last[:, C // 2 :], start=False, stop=True)
-        nc.vector.tensor_tensor(s_early[:], ex[1][:], e1_last[:, : C // 2], ALU.add)
+        weights32 = d1_first[:, :P]
+        nc.vector.tensor_copy(weights32, weights[:])
+        nc.vector.tensor_tensor(s_last[:], ex[1][:], e1_last, ALU.add)
 
-        parts_in_turn = [(early, s_early), (first, ex[0]), (late, ex[2])]
+        parts_in_turn = [(last, s_last), (first, ex[0])]
         pieces = [slice(c, c + W) for cols, sums in parts_in_turn for c in range(cols.start, cols.stop, W)]
         sums = [sums[:, c : c + W] for cols, sums in parts_in_turn for c in range(0, cols.stop - cols.start, W)]
-        exact = [0, 2, 4]
-        nc.scalar.copy(weights32[:], weights[:])
+        exact = [0, 1]
         products = {}
         for i in exact:
             products[i] = ring.tile([P, W], F32, name="product", tag="bank")
-            nc.tensor.matmul(products[i][:], weights32[:], h(pieces[i]), start=True, stop=False)
+            nc.tensor.matmul(products[i][:], weights32, h(pieces[i]), start=True, stop=False)
         for i in range(len(pieces)):
             nc.scalar.activation(logs[:, i * W : (i + 1) * W], sums[i], ACT.Ln)
         for i, piece in enumerate(pieces):
             if i in exact:
-                nc.tensor.matmul(products[i][:], weights32[:], logs[:, i * W : (i + 1) * W], start=False, stop=True)
+                nc.tensor.matmul(products[i][:], weights32, logs[:, i * W : (i + 1) * W], start=False, stop=True)
             else:
                 products[i] = ring.tile([P, W], F32, name="product", tag="bank")
                 nc.vector.tensor_tensor(x[:, piece], h(piece), logs[:, i * W : (i + 1) * W], ALU.add)
                 nc.tensor.matmul(products[i][:], weights[:], x[:, piece], start=True, stop=True)
-        results = [h_swapped[:, C + W : C + 3 * W], h_swapped[:, C - W : C + W], logs[:, V - W :], m0[:, : 2 * W]]
         for i, piece in enumerate(pieces):
-            result = results[i // 2][:, i % 2 * W : (i % 2 + 1) * W]
-            if i in (1, 3, 5, 6):
-                nc.scalar.activation(result, products[i][:], ACT.Relu, bias=bias[:, 0:1])
+            if i < 3 or i % 2 == 0:
+                nc.scalar.activation(result[:, piece], products[i][:], ACT.Relu, bias=bias[:, 0:1])
             else:
-                nc.vector.tensor_scalar(result, products[i][:], bias[:, 0:1], 0.0, ALU.add, ALU.max)
+                nc.vector.tensor_scalar(result[:, piece], products[i][:], bias[:, 0:1], 0.0, ALU.add, ALU.max)
             if i % 2 == 1:
-                nc.sync.dma_start(out[:, piece.start - W : piece.stop], results[i // 2])
+                nc.sync.dma_start(out[:, piece.start - W : piece.stop], result[:, piece.start - W : piece.stop])

@@ -26,7 +26,7 @@ def tile_lookup_lse_relu_kernel(tc, tab, x0, w, b, offs, out):
     nc = tc.nc
     with (
         tc.tile_pool(name="held", bufs=1) as held,
-        tc.psum_pool(name="ring", bufs=8) as ring,
+        tc.psum_pool(name="psum", bufs=1) as psum,
     ):
         first, last = slice(0, C), slice(C, V)
         chunks = [first, last]
@@ -71,8 +71,8 @@ def tile_lookup_lse_relu_kernel(tc, tab, x0, w, b, offs, out):
         logs = held.tile([P, V], F32, name="logs")
         result = held.tile([P, V], F32, name="result")
         x = held.tile([P, V], BF16, name="x")
-        dx = [ring.tile([P, C], F32, name=f"dx{c}", tag="bank") for c in range(len(chunks))]
-        ex = [ring.tile([P, C], F32, name=f"ex{c}", tag="bank") for c in range(len(chunks))]
+        dx = [psum.tile([P, C], F32, name=f"dx{c}") for c in range(len(chunks))]
+        ex = [psum.tile([P, C], F32, name=f"ex{c}") for c in range(len(chunks))]
 
         for cols in chunks:
             nc.vector.tensor_tensor(m0[:, cols], table[:].indirect(entries(offsets, 0, cols)), node[:, cols], ALU.max)
@@ -95,6 +95,18 @@ def tile_lookup_lse_relu_kernel(tc, tab, x0, w, b, offs, out):
         for bank, cols in zip(ex, chunks):
             add_transposed(bank, ex_t[:, cols], start=True, stop=False)
 
+        parts_in_turn = [(last, s_last), (first, ex[0])]
+        pieces = [slice(c, c + W) for cols, sums in parts_in_turn for c in range(cols.start, cols.stop, W)]
+        sums = [sums[:, c : c + W] for cols, sums in parts_in_turn for c in range(0, cols.stop - cols.start, W)]
+        exact = [0, 1]
+        banks = ["dx0", "dx1", "free0", "free1", "free2", "free3", "ex1", "ex0"]
+        weights32 = held.tile([P, P], F32, name="weights32")
+        nc.scalar.copy(weights32[:], weights[:])
+        products = {}
+        for i in exact:
+            products[i] = psum.tile([P, W], F32, name=f"product{i}", tag=banks[i])
+            nc.tensor.matmul(products[i][:], weights32[:], h(pieces[i]), start=True, stop=False)
+
         e0_first, e0_last = ex_t[:, first], front[:, :C]
         e1_first, e1_last = front[:, C:], d0_last
         nc.scalar.activation(e0_first, d0_first, ACT.Exp)
@@ -105,25 +117,15 @@ def tile_lookup_lse_relu_kernel(tc, tab, x0, w, b, offs, out):
         nc.tensor.matmul(ex[0][:], identity[:], e0_first, start=False, stop=False)
         nc.tensor.matmul(ex[1][:], identity[:], e0_last, start=False, stop=True)
         nc.tensor.matmul(ex[0][:], identity[:], e1_first, start=False, stop=True)
-        weights32 = d1_first[:, :P]
-        nc.vector.tensor_copy(weights32, weights[:])
         nc.vector.tensor_tensor(s_last[:], ex[1][:], e1_last, ALU.add)
 
-        parts_in_turn = [(last, s_last), (first, ex[0])]
-        pieces = [slice(c, c + W) for cols, sums in parts_in_turn for c in range(cols.start, cols.stop, W)]
-        sums = [sums[:, c : c + W] for cols, sums in parts_in_turn for c in range(0, cols.stop - cols.start, W)]
-        exact = [0, 1]
-        products = {}
-        for i in exact:
-            products[i] = ring.tile([P, W], F32, name="product", tag="bank")
-            nc.tensor.matmul(products[i][:], weights32, h(pieces[i]), start=True, stop=False)
         for i in range(len(pieces)):
             nc.scalar.activation(logs[:, i * W : (i + 1) * W], sums[i], ACT.Ln)
         for i, piece in enumerate(pieces):
             if i in exact:
-                nc.tensor.matmul(products[i][:], weights32, logs[:, i * W : (i + 1) * W], start=False, stop=True)
+                nc.tensor.matmul(products[i][:], weights32[:], logs[:, i * W : (i + 1) * W], start=False, stop=True)
             else:
-                products[i] = ring.tile([P, W], F32, name="product", tag="bank")
+                products[i] = psum.tile([P, W], F32, name=f"product{i}", tag=banks[i])
                 nc.vector.tensor_tensor(x[:, piece], h(piece), logs[:, i * W : (i + 1) * W], ALU.add)
                 nc.tensor.matmul(products[i][:], weights[:], x[:, piece], start=True, stop=True)
         for i, piece in enumerate(pieces):

@@ -117,7 +117,8 @@ def tile_lookup_lse_relu_kernel(tc, tab, x0, w, b, offs, out):
         nc.tensor.matmul(ex[0][:], identity[:], e0_first, start=False, stop=False)
         nc.tensor.matmul(ex[1][:], identity[:], e0_last, start=False, stop=True)
         nc.tensor.matmul(ex[0][:], identity[:], e1_first, start=False, stop=True)
-        nc.vector.tensor_tensor(s_last[:], ex[1][:], e1_last, ALU.add)
+        for half in [slice(0, C // 2), slice(C // 2, C)]:
+            nc.vector.tensor_tensor(s_last[:, half], ex[1][:, half], e1_last[:, half], ALU.add)
 
         for i in range(len(pieces)):
             nc.scalar.activation(logs[:, i * W : (i + 1) * W], sums[i], ACT.Ln)

@@ -11,15 +11,11 @@ S = 2048
 N = 2 * V
 C = 512
 PER = 16
-
 SPLIT = (S - C) // 2
+W = 128
+SCALAR_ALONE = 3
 
 FLOPS = 2 * P * P * V
-W = 128
-
-
-def entries(offsets, d, cols):
-    return offsets[:, (d * V + cols.start) // PER : (d * V + cols.stop) // PER]
 
 
 def tile_lookup_lse_relu_kernel(tc, tab, x0, w, b, offs, out):
@@ -47,6 +43,9 @@ def tile_lookup_lse_relu_kernel(tc, tab, x0, w, b, offs, out):
         identity = held.tile([P, P], F32, name="identity")
         make_identity(nc, identity[:])
 
+        def picked(start, stop):
+            return table[:].indirect(offsets[:, start // PER : stop // PER])
+
         def add_transposed(bank, source, start, stop):
             blocks = source.shape[1] // P
             for k in range(blocks):
@@ -54,85 +53,64 @@ def tile_lookup_lse_relu_kernel(tc, tab, x0, w, b, offs, out):
                 nc.tensor.matmul(bank[:, block], source[:, block], identity[:], is_transpose=True,
                                  start=start and k == 0, stop=stop and k == blocks - 1)
 
-        m0 = held.tile([P, V], F32, name="m0")
+        m = held.tile([P, V], F32, name="m")
         h_swapped = held.tile([P, V], F32, name="h_swapped")
-        front = held.tile([P, V], F32, name="front")
-        middle = held.tile([P, V], F32, name="middle")
-        d1_last = held.tile([P, C], F32, name="d1_last")
-        d0_first, d0_last, d1_first = front[:, C // 2 : C // 2 + C], middle[:, :C], middle[:, C:]
+        shared = held.tile([P, V + C], F32, name="shared")
+        later = held.tile([P, V + C], F32, name="later")
 
         def h(cols):
             start = (cols.start + C) % V
             return h_swapped[:, start : start + cols.stop - cols.start]
 
+        for cols in chunks:
+            nc.vector.tensor_tensor(m[:, cols], picked(cols.start, cols.stop), node[:, cols], ALU.max)
+        for cols in chunks:
+            nc.vector.tensor_tensor(h(cols), picked(V + cols.start, V + cols.stop), m[:, cols], ALU.max)
+        parts = [(slice(0, C), h(first)), (slice(C, N - C), h_swapped[:]), (slice(N - C, N), h(last))]
+        diffs = [shared[:, V - C // 2 : V + C // 2], later[:, :V], later[:, V:]]
+        for (part, maxima), diff in zip(parts, diffs):
+            nc.vector.tensor_tensor(diff, picked(part.start, part.stop), maxima, ALU.subtract)
+
         negated = held.tile([P, V], F32, name="negated")
-        ex_t = held.tile([P, V], F32, name="ex_t")
-        s_last = held.tile([P, C], F32, name="s_last")
-        logs = held.tile([P, V], F32, name="logs")
-        result = held.tile([P, V], F32, name="result")
-        x = held.tile([P, V], BF16, name="x")
-        dx = [psum.tile([P, C], F32, name=f"dx{c}") for c in range(len(chunks))]
-        ex = [psum.tile([P, C], F32, name=f"ex{c}") for c in range(len(chunks))]
-
-        for cols in chunks:
-            nc.vector.tensor_tensor(m0[:, cols], table[:].indirect(entries(offsets, 0, cols)), node[:, cols], ALU.max)
-        for cols in chunks:
-            nc.vector.tensor_tensor(h(cols), table[:].indirect(entries(offsets, 1, cols)), m0[:, cols], ALU.max)
-        for diffs, part, maxima in [
-            (d0_first, slice(0, C), h(first)),
-            (middle[:], slice(C, N - C), h_swapped[:, :V]),
-            (d1_last[:], slice(N - C, N), h(last)),
-        ]:
-            nc.vector.tensor_tensor(diffs, table[:].indirect(entries(offsets, 0, part)), maxima, ALU.subtract)
-
+        own_t = held.tile([P, V], F32, name="own_t")
+        gaps = [psum.tile([P, C], F32, name=f"gap{c}") for c in range(len(chunks))]
+        own = [psum.tile([P, C], F32, name=f"own{c}") for c in range(len(chunks))]
         for cols in chunks:
             nc.scalar.mul(negated[:, cols], node[:, cols], -1.0)
         for c, cols in enumerate(chunks):
-            add_transposed(dx[c], negated[:, cols], start=True, stop=False)
+            add_transposed(gaps[c], negated[:, cols], start=True, stop=False)
         for c, cols in enumerate(chunks):
-            add_transposed(dx[c], h(cols), start=False, stop=True)
-            nc.scalar.activation(ex_t[:, cols], dx[c][:], ACT.Exp, scale=-1.0)
-        for bank, cols in zip(ex, chunks):
-            add_transposed(bank, ex_t[:, cols], start=True, stop=False)
+            add_transposed(gaps[c], h(cols), start=False, stop=True)
+            nc.scalar.activation(own_t[:, cols], gaps[c][:], ACT.Exp, scale=-1.0)
+        add_transposed(own[0], own_t[:, first], start=True, stop=False)
+        add_transposed(own[1], own_t[:, last], start=True, stop=True)
+        terms = [own_t[:, C // 2 : C // 2 + C], shared[:, :V], shared[:, V:]]
+        for diff, term in zip(diffs, terms):
+            nc.scalar.activation(term, diff, ACT.Exp)
+        e0_first, e0_last, e1_first, e1_last = terms[0], terms[1][:, :C], terms[1][:, C:], terms[2]
 
-        parts_in_turn = [(last, s_last), (first, ex[0])]
-        pieces = [slice(c, c + W) for cols, sums in parts_in_turn for c in range(cols.start, cols.stop, W)]
-        sums = [sums[:, c : c + W] for cols, sums in parts_in_turn for c in range(0, cols.stop - cols.start, W)]
-        exact = [0, 1]
-        banks = ["dx0", "dx1", "free0", "free1", "free2", "free3", "ex1", "ex0"]
-        weights32 = held.tile([P, P], F32, name="weights32")
-        nc.scalar.copy(weights32[:], weights[:])
-        products = {}
-        for i in exact:
-            products[i] = psum.tile([P, W], F32, name=f"product{i}", tag=banks[i])
-            nc.tensor.matmul(products[i][:], weights32[:], h(pieces[i]), start=True, stop=False)
+        partial = held.tile([P, C], F32, name="partial")
+        sums = held.tile([P, V], F32, name="sums")
+        nc.tensor.matmul(own[0][:], identity[:], e0_first, start=False, stop=True)
+        nc.vector.tensor_tensor(partial[:], own[1][:], e0_last, ALU.add)
+        nc.vector.tensor_tensor(sums[:, first], own[0][:], e1_first, ALU.add)
+        nc.vector.tensor_tensor(sums[:, last], partial[:], e1_last, ALU.add)
 
-        e0_first, e0_last = ex_t[:, first], front[:, :C]
-        e1_first, e1_last = front[:, C:], d0_last
-        nc.scalar.activation(e0_first, d0_first, ACT.Exp)
-        nc.scalar.activation(e0_last, d0_last, ACT.Exp)
-        nc.scalar.activation(e1_first, d1_first, ACT.Exp)
-        nc.scalar.activation(e1_last, d1_last[:], ACT.Exp)
-
-        nc.tensor.matmul(ex[0][:], identity[:], e0_first, start=False, stop=False)
-        nc.tensor.matmul(ex[1][:], identity[:], e0_last, start=False, stop=True)
-        nc.tensor.matmul(ex[0][:], identity[:], e1_first, start=False, stop=True)
-        for half in [slice(0, C // 2), slice(C // 2, C)]:
-            nc.vector.tensor_tensor(s_last[:, half], ex[1][:, half], e1_last[:, half], ALU.add)
-
-        for i in range(len(pieces)):
-            nc.scalar.activation(logs[:, i * W : (i + 1) * W], sums[i], ACT.Ln)
-        for i, piece in enumerate(pieces):
-            if i in exact:
-                nc.tensor.matmul(products[i][:], weights32[:], logs[:, i * W : (i + 1) * W], start=False, stop=True)
+        logs = held.tile([P, V], F32, name="logs")
+        x = held.tile([P, V], BF16, name="x")
+        result = held.tile([P, V], F32, name="result")
+        pieces = [slice(c, c + W) for c in range(0, V, W)]
+        banks = ["free0", "free1", "free2", "free3", "gap0", "gap1", "own0", "own1"]
+        products = [psum.tile([P, W], F32, name=f"product{i}", tag=bank) for i, bank in enumerate(banks)]
+        for piece in pieces:
+            nc.scalar.activation(logs[:, piece], sums[:, piece], ACT.Ln)
+        for piece, product in zip(pieces, products):
+            nc.vector.tensor_tensor(x[:, piece], h(piece), logs[:, piece], ALU.add)
+            nc.tensor.matmul(product[:], weights[:], x[:, piece], start=True, stop=True)
+        for i, (piece, product) in enumerate(zip(pieces, products)):
+            if i < SCALAR_ALONE or i % 2 == 0:
+                nc.scalar.activation(result[:, piece], product[:], ACT.Relu, bias=bias[:, 0:1])
             else:
-                products[i] = psum.tile([P, W], F32, name=f"product{i}", tag=banks[i])
-                nc.vector.tensor_tensor(x[:, piece], h(piece), logs[:, i * W : (i + 1) * W], ALU.add)
-                nc.tensor.matmul(products[i][:], weights[:], x[:, piece], start=True, stop=True)
-        for i, piece in enumerate(pieces):
-            if i < 3 or i % 2 == 0:
-                nc.scalar.activation(result[:, piece], products[i][:], ACT.Relu, bias=bias[:, 0:1])
-            else:
-                nc.vector.tensor_scalar(result[:, piece], products[i][:], bias[:, 0:1], 0.0, ALU.add, ALU.max)
+                nc.vector.tensor_scalar(result[:, piece], product[:], bias[:, 0:1], 0.0, ALU.add, ALU.max)
             if i % 2 == 1:
                 nc.sync.dma_start(out[:, piece.start - W : piece.stop], result[:, piece.start - W : piece.stop])

@@ -13,6 +13,7 @@ C = 512
 PER = 16
 SPLIT = (S - C) // 2
 W = 128
+EXACT = 2
 SCALAR_ALONE = 3
 
 FLOPS = 2 * P * P * V
@@ -74,7 +75,9 @@ def tile_lookup_lse_relu_kernel(tc, tab, x0, w, b, offs, out):
         negated = held.tile([P, V], F32, name="negated")
         own_t = held.tile([P, V], F32, name="own_t")
         gaps = [psum.tile([P, C], F32, name=f"gap{c}") for c in range(len(chunks))]
-        own = [psum.tile([P, C], F32, name=f"own{c}") for c in range(len(chunks))]
+        early, late = slice(0, C // 2), slice(C // 2, C)
+        owned = [first, slice(C, C + C // 2), slice(C + C // 2, V)]
+        own = [psum.tile([P, cols.stop - cols.start], F32, name=f"own{c}") for c, cols in enumerate(owned)]
         for cols in chunks:
             nc.scalar.mul(negated[:, cols], node[:, cols], -1.0)
         for c, cols in enumerate(chunks):
@@ -82,29 +85,37 @@ def tile_lookup_lse_relu_kernel(tc, tab, x0, w, b, offs, out):
         for c, cols in enumerate(chunks):
             add_transposed(gaps[c], h(cols), start=False, stop=True)
             nc.scalar.activation(own_t[:, cols], gaps[c][:], ACT.Exp, scale=-1.0)
-        add_transposed(own[0], own_t[:, first], start=True, stop=False)
-        add_transposed(own[1], own_t[:, last], start=True, stop=True)
-        terms = [own_t[:, C // 2 : C // 2 + C], shared[:, :V], shared[:, V:]]
+        for bank, cols in zip(own, owned):
+            add_transposed(bank, own_t[:, cols], start=True, stop=cols == owned[1])
+        terms = [own_t[:, first], shared[:, :V], shared[:, V : V + C]]
         for diff, term in zip(diffs, terms):
             nc.scalar.activation(term, diff, ACT.Exp)
         e0_first, e0_last, e1_first, e1_last = terms[0], terms[1][:, :C], terms[1][:, C:], terms[2]
 
-        partial = held.tile([P, C], F32, name="partial")
         sums = held.tile([P, V], F32, name="sums")
         nc.tensor.matmul(own[0][:], identity[:], e0_first, start=False, stop=True)
-        nc.vector.tensor_tensor(partial[:], own[1][:], e0_last, ALU.add)
+        nc.tensor.matmul(own[2][:], identity[:], e0_last[:, late], start=False, stop=True)
+        partial = held.tile([P, C // 2], F32, name="partial")
+        nc.vector.tensor_tensor(partial[:], own[1][:], e0_last[:, early], ALU.add)
         nc.vector.tensor_tensor(sums[:, first], own[0][:], e1_first, ALU.add)
-        nc.vector.tensor_tensor(sums[:, last], partial[:], e1_last, ALU.add)
+        nc.vector.tensor_tensor(sums[:, owned[1]], partial[:], e1_last[:, early], ALU.add)
+        nc.vector.tensor_tensor(sums[:, owned[2]], own[2][:], e1_last[:, late], ALU.add)
 
         logs = held.tile([P, V], F32, name="logs")
-        x = held.tile([P, V], BF16, name="x")
+        x = held.tile([P, V], BF16, name="x", tag="shared")
         result = held.tile([P, V], F32, name="result")
         pieces = [slice(c, c + W) for c in range(0, V, W)]
-        banks = ["free0", "free1", "free2", "free3", "gap0", "gap1", "own0", "own1"]
+        banks = ["gap0", "gap1", "free0", "free1", "free2", "own0", "own1", "own2"]
         products = [psum.tile([P, W], F32, name=f"product{i}", tag=bank) for i, bank in enumerate(banks)]
+        weights32 = held.tile([P, P], F32, name="weights32", tag="partial")
+        nc.vector.tensor_copy(weights32[:], weights[:])
+        for piece, product in zip(pieces[:EXACT], products):
+            nc.tensor.matmul(product[:], weights32[:], h(piece), start=True, stop=False)
         for piece in pieces:
             nc.scalar.activation(logs[:, piece], sums[:, piece], ACT.Ln)
-        for piece, product in zip(pieces, products):
+        for piece, product in zip(pieces[:EXACT], products):
+            nc.tensor.matmul(product[:], weights32[:], logs[:, piece], start=False, stop=True)
+        for piece, product in zip(pieces[EXACT:], products[EXACT:]):
             nc.vector.tensor_tensor(x[:, piece], h(piece), logs[:, piece], ALU.add)
             nc.tensor.matmul(product[:], weights[:], x[:, piece], start=True, stop=True)
         for i, (piece, product) in enumerate(zip(pieces, products)):

@@ -13,7 +13,6 @@ C = 512
 PER = 16
 SPLIT = (S - C) // 2
 W = 128
-EXACT = 2
 SCALAR_ALONE = 3
 
 FLOPS = 2 * P * P * V
@@ -44,8 +43,8 @@ def tile_lookup_lse_relu_kernel(tc, tab, x0, w, b, offs, out):
         identity = held.tile([P, P], F32, name="identity")
         make_identity(nc, identity[:])
 
-        def picked(start, stop):
-            return table[:].indirect(offsets[:, start // PER : stop // PER])
+        def picked(d, cols):
+            return table[:].indirect(offsets[:, (d * V + cols.start) // PER : (d * V + cols.stop) // PER])
 
         def add_transposed(bank, source, start, stop):
             blocks = source.shape[1] // P
@@ -55,68 +54,60 @@ def tile_lookup_lse_relu_kernel(tc, tab, x0, w, b, offs, out):
                                  start=start and k == 0, stop=stop and k == blocks - 1)
 
         m = held.tile([P, V], F32, name="m")
-        h_swapped = held.tile([P, V], F32, name="h_swapped")
+        h = held.tile([P, V], F32, name="h")
         shared = held.tile([P, V + C], F32, name="shared")
         later = held.tile([P, V + C], F32, name="later")
-
-        def h(cols):
-            start = (cols.start + C) % V
-            return h_swapped[:, start : start + cols.stop - cols.start]
-
         for cols in chunks:
-            nc.vector.tensor_tensor(m[:, cols], picked(cols.start, cols.stop), node[:, cols], ALU.max)
+            nc.vector.tensor_tensor(m[:, cols], picked(0, cols), node[:, cols], ALU.max)
         for cols in chunks:
-            nc.vector.tensor_tensor(h(cols), picked(V + cols.start, V + cols.stop), m[:, cols], ALU.max)
-        parts = [(slice(0, C), h(first)), (slice(C, N - C), h_swapped[:]), (slice(N - C, N), h(last))]
-        diffs = [shared[:, V - C // 2 : V + C // 2], later[:, :V], later[:, V:]]
-        for (part, maxima), diff in zip(parts, diffs):
-            nc.vector.tensor_tensor(diff, picked(part.start, part.stop), maxima, ALU.subtract)
+            nc.vector.tensor_tensor(h[:, cols], picked(1, cols), m[:, cols], ALU.max)
+        d1_first, d0, d1_last = shared[:, V - C // 2 : V + C // 2], later[:, :V], later[:, V:]
+        nc.vector.tensor_tensor(d1_first, picked(1, first), h[:, first], ALU.subtract)
+        nc.vector.tensor_tensor(d0, picked(0, slice(0, V)), h[:], ALU.subtract)
+        nc.vector.tensor_tensor(d1_last, picked(1, last), h[:, last], ALU.subtract)
 
         negated = held.tile([P, V], F32, name="negated")
         own_t = held.tile([P, V], F32, name="own_t")
+        third, fourth = slice(C, C + C // 2), slice(C + C // 2, V)
         gaps = [psum.tile([P, C], F32, name=f"gap{c}") for c in range(len(chunks))]
-        early, late = slice(0, C // 2), slice(C // 2, C)
-        owned = [first, slice(C, C + C // 2), slice(C + C // 2, V)]
-        own = [psum.tile([P, cols.stop - cols.start], F32, name=f"own{c}") for c, cols in enumerate(owned)]
+        open_first = psum.tile([P, C], F32, name="open_first")
+        open_third = psum.tile([P, C // 2], F32, name="open_third")
+        open_fourth = psum.tile([P, C // 2], F32, name="open_fourth")
         for cols in chunks:
             nc.scalar.mul(negated[:, cols], node[:, cols], -1.0)
-        for c, cols in enumerate(chunks):
-            add_transposed(gaps[c], negated[:, cols], start=True, stop=False)
-        for c, cols in enumerate(chunks):
-            add_transposed(gaps[c], h(cols), start=False, stop=True)
-            nc.scalar.activation(own_t[:, cols], gaps[c][:], ACT.Exp, scale=-1.0)
-        for bank, cols in zip(own, owned):
-            add_transposed(bank, own_t[:, cols], start=True, stop=cols == owned[1])
-        terms = [own_t[:, first], shared[:, :V], shared[:, V : V + C]]
-        for diff, term in zip(diffs, terms):
-            nc.scalar.activation(term, diff, ACT.Exp)
-        e0_first, e0_last, e1_first, e1_last = terms[0], terms[1][:, :C], terms[1][:, C:], terms[2]
+        for gap, cols in zip(gaps, chunks):
+            add_transposed(gap, negated[:, cols], start=True, stop=False)
+        for gap, cols in zip(gaps, chunks):
+            add_transposed(gap, h[:, cols], start=False, stop=True)
+            nc.scalar.activation(own_t[:, cols], gap[:], ACT.Exp, scale=-1.0)
+        add_transposed(open_first, own_t[:, first], start=True, stop=False)
+        add_transposed(open_third, own_t[:, third], start=True, stop=True)
+        add_transposed(open_fourth, own_t[:, fourth], start=True, stop=False)
+
+        e1_first, e0, e1_last = own_t[:, first], shared[:, :V], shared[:, V:]
+        nc.scalar.activation(e1_first, d1_first, ACT.Exp)
+        nc.scalar.activation(e0, d0, ACT.Exp)
+        nc.scalar.activation(e1_last, d1_last, ACT.Exp)
 
         sums = held.tile([P, V], F32, name="sums")
-        nc.tensor.matmul(own[0][:], identity[:], e0_first, start=False, stop=True)
-        nc.tensor.matmul(own[2][:], identity[:], e0_last[:, late], start=False, stop=True)
         partial = held.tile([P, C // 2], F32, name="partial")
-        nc.vector.tensor_tensor(partial[:], own[1][:], e0_last[:, early], ALU.add)
-        nc.vector.tensor_tensor(sums[:, first], own[0][:], e1_first, ALU.add)
-        nc.vector.tensor_tensor(sums[:, owned[1]], partial[:], e1_last[:, early], ALU.add)
-        nc.vector.tensor_tensor(sums[:, owned[2]], own[2][:], e1_last[:, late], ALU.add)
+        nc.tensor.matmul(open_first[:], identity[:], e1_first, start=False, stop=True)
+        nc.tensor.matmul(open_fourth[:], identity[:], e0[:, fourth], start=False, stop=True)
+        nc.vector.tensor_tensor(partial[:], open_third[:], e0[:, third], ALU.add)
+        nc.vector.tensor_tensor(sums[:, first], open_first[:], e0[:, first], ALU.add)
+        nc.vector.tensor_tensor(sums[:, third], partial[:], e1_last[:, : C // 2], ALU.add)
+        nc.vector.tensor_tensor(sums[:, fourth], open_fourth[:], e1_last[:, C // 2 :], ALU.add)
 
-        logs = held.tile([P, V], F32, name="logs")
-        x = held.tile([P, V], BF16, name="x", tag="shared")
-        result = held.tile([P, V], F32, name="result")
         pieces = [slice(c, c + W) for c in range(0, V, W)]
-        banks = ["gap0", "gap1", "free0", "free1", "free2", "own0", "own1", "own2"]
+        banks = ["gap0", "gap1", "free0", "free1", "free2", "open_first", "open_third", "open_fourth"]
         products = [psum.tile([P, W], F32, name=f"product{i}", tag=bank) for i, bank in enumerate(banks)]
-        weights32 = held.tile([P, P], F32, name="weights32", tag="partial")
-        nc.vector.tensor_copy(weights32[:], weights[:])
-        for piece, product in zip(pieces[:EXACT], products):
-            nc.tensor.matmul(product[:], weights32[:], h(piece), start=True, stop=False)
+        logs = held.tile([P, V], F32, name="logs")
+        result = held.tile([P, V], F32, name="result")
+        x = held.tile([P, V], BF16, name="x", tag="shared")
         for piece in pieces:
             nc.scalar.activation(logs[:, piece], sums[:, piece], ACT.Ln)
-        for piece, product in zip(pieces[:EXACT], products):
-            nc.tensor.matmul(product[:], weights32[:], logs[:, piece], start=False, stop=True)
-        for piece, product in zip(pieces[EXACT:], products[EXACT:]):
-            nc.vector.tensor_tensor(x[:, piece], h(piece), logs[:, piece], ALU.add)
+        for piece, product in zip(pieces, products):
+            nc.vector.tensor_tensor(x[:, piece], h[:, piece], logs[:, piece], ALU.add)
             nc.tensor.matmul(product[:], weights[:], x[:, piece], start=True, stop=True)
         for i, (piece, product) in enumerate(zip(pieces, products)):
             if i < SCALAR_ALONE or i % 2 == 0:

@@ -68,11 +68,9 @@ def tile_lookup_lse_relu_kernel(tc, tab, x0, w, b, offs, out):
 
         negated = held.tile([P, V], F32, name="negated")
         own_t = held.tile([P, V], F32, name="own_t")
-        third, fourth = slice(C, C + C // 2), slice(C + C // 2, V)
+        parts = [first, slice(C, C + C // 2), slice(C + C // 2, V)]
         gaps = [psum.tile([P, C], F32, name=f"gap{c}") for c in range(len(chunks))]
-        open_first = psum.tile([P, C], F32, name="open_first")
-        open_third = psum.tile([P, C // 2], F32, name="open_third")
-        open_fourth = psum.tile([P, C // 2], F32, name="open_fourth")
+        opened = [psum.tile([P, cols.stop - cols.start], F32, name=f"opened{c}") for c, cols in enumerate(parts)]
         for cols in chunks:
             nc.scalar.mul(negated[:, cols], node[:, cols], -1.0)
         for gap, cols in zip(gaps, chunks):
@@ -80,9 +78,8 @@ def tile_lookup_lse_relu_kernel(tc, tab, x0, w, b, offs, out):
         for gap, cols in zip(gaps, chunks):
             add_transposed(gap, h[:, cols], start=False, stop=True)
             nc.scalar.activation(own_t[:, cols], gap[:], ACT.Exp, scale=-1.0)
-        add_transposed(open_first, own_t[:, first], start=True, stop=False)
-        add_transposed(open_third, own_t[:, third], start=True, stop=True)
-        add_transposed(open_fourth, own_t[:, fourth], start=True, stop=False)
+        for bank, cols in zip(opened, parts):
+            add_transposed(bank, own_t[:, cols], start=True, stop=False)
 
         e1_first, e0, e1_last = own_t[:, first], shared[:, :V], shared[:, V:]
         nc.scalar.activation(e1_first, d1_first, ACT.Exp)
@@ -90,16 +87,14 @@ def tile_lookup_lse_relu_kernel(tc, tab, x0, w, b, offs, out):
         nc.scalar.activation(e1_last, d1_last, ACT.Exp)
 
         sums = held.tile([P, V], F32, name="sums")
-        partial = held.tile([P, C // 2], F32, name="partial")
-        nc.tensor.matmul(open_first[:], identity[:], e1_first, start=False, stop=True)
-        nc.tensor.matmul(open_fourth[:], identity[:], e0[:, fourth], start=False, stop=True)
-        nc.vector.tensor_tensor(partial[:], open_third[:], e0[:, third], ALU.add)
-        nc.vector.tensor_tensor(sums[:, first], open_first[:], e0[:, first], ALU.add)
-        nc.vector.tensor_tensor(sums[:, third], partial[:], e1_last[:, : C // 2], ALU.add)
-        nc.vector.tensor_tensor(sums[:, fourth], open_fourth[:], e1_last[:, C // 2 :], ALU.add)
+        on_tensor = [e1_first, e0[:, parts[1]], e1_last[:, C // 2 :]]
+        on_vector = [e0[:, first], e1_last[:, : C // 2], e0[:, parts[2]]]
+        for bank, cols, one, other in zip(opened, parts, on_tensor, on_vector):
+            nc.tensor.matmul(bank[:], identity[:], one, start=False, stop=True)
+            nc.vector.tensor_tensor(sums[:, cols], bank[:], other, ALU.add)
 
         pieces = [slice(c, c + W) for c in range(0, V, W)]
-        banks = ["gap0", "gap1", "free0", "free1", "free2", "open_first", "open_third", "open_fourth"]
+        banks = ["gap0", "gap1", "free0", "free1", "free2", "opened0", "opened1", "opened2"]
         products = [psum.tile([P, W], F32, name=f"product{i}", tag=bank) for i, bank in enumerate(banks)]
         logs = held.tile([P, V], F32, name="logs")
         result = held.tile([P, V], F32, name="result")

@@ -13,6 +13,7 @@ C = 512
 PER = 16
 SPLIT = (S - C) // 2
 W = 128
+EXACT = 2
 SCALAR_ALONE = 3
 
 FLOPS = 2 * P * P * V
@@ -94,14 +95,20 @@ def tile_lookup_lse_relu_kernel(tc, tab, x0, w, b, offs, out):
             nc.vector.tensor_tensor(sums[:, cols], bank[:], other, ALU.add)
 
         pieces = [slice(c, c + W) for c in range(0, V, W)]
-        banks = ["gap0", "gap1", "free0", "free1", "free2", "opened0", "opened1", "opened2"]
+        banks = ["opened0", "opened1", "free0", "free1", "free2", "gap0", "gap1", "opened2"]
         products = [psum.tile([P, W], F32, name=f"product{i}", tag=bank) for i, bank in enumerate(banks)]
         logs = held.tile([P, V], F32, name="logs")
         result = held.tile([P, V], F32, name="result")
         x = held.tile([P, V], BF16, name="x", tag="shared")
+        weights32 = held.tile([P, P], F32, name="weights32")
+        nc.scalar.copy(weights32[:], weights[:])
+        for piece, product in zip(pieces[:EXACT], products):
+            nc.tensor.matmul(product[:], weights32[:], h[:, piece], start=True, stop=False)
         for piece in pieces:
             nc.scalar.activation(logs[:, piece], sums[:, piece], ACT.Ln)
-        for piece, product in zip(pieces, products):
+        for piece, product in zip(pieces[:EXACT], products):
+            nc.tensor.matmul(product[:], weights32[:], logs[:, piece], start=False, stop=True)
+        for piece, product in zip(pieces[EXACT:], products[EXACT:]):
             nc.vector.tensor_tensor(x[:, piece], h[:, piece], logs[:, piece], ALU.add)
             nc.tensor.matmul(product[:], weights[:], x[:, piece], start=True, stop=True)
         for i, (piece, product) in enumerate(zip(pieces, products)):

@@ -1,5 +1,4 @@
 import concourse.mybir as mybir
-from concourse.masks import make_identity
 
 F32, BF16, U16 = mybir.dt.float32, mybir.dt.bfloat16, mybir.dt.uint16
 ALU = mybir.AluOpType
@@ -10,11 +9,11 @@ V = 1024
 S = 2048
 N = 2 * V
 C = 512
+Q = 32
 PER = 16
 SPLIT = (S - C) // 2
 W = 128
-EXACT = 2
-SCALAR_ALONE = 3
+BOUND = 32.0
 
 FLOPS = 2 * P * P * V
 
@@ -41,8 +40,16 @@ def tile_lookup_lse_relu_kernel(tc, tab, x0, w, b, offs, out):
         nc.sync.dma_start(weights[:], w)
         nc.sync.dma_start(bias[:], b)
 
+        ones = held.tile([P, Q], F32, name="ones")
+        column = held.tile([P, Q], F32, name="column", align_bytes=64)
+        row = held.tile([P, Q], F32, name="row", align_bytes=64)
         identity = held.tile([P, P], F32, name="identity")
-        make_identity(nc, identity[:])
+        nc.vector.memset(ones[:], 1.0)
+        nc.vector.memset(identity[:], 0.0)
+        nc.vector.tensor_tensor_scan(column[:], ones[:], ones[:], 0.0, ALU.mult, ALU.add)
+        nc.vector.transpose(row[:], column[:])
+        for q in range(0, P, Q):
+            nc.vector.tensor_tensor(identity[q : q + Q, q : q + Q], column[q : q + Q, :], row[q : q + Q, :], ALU.is_equal)
 
         def picked(d, cols):
             return table[:].indirect(offsets[:, (d * V + cols.start) // PER : (d * V + cols.stop) // PER])
@@ -56,65 +63,90 @@ def tile_lookup_lse_relu_kernel(tc, tab, x0, w, b, offs, out):
 
         m = held.tile([P, V], F32, name="m")
         h = held.tile([P, V], F32, name="h")
-        shared = held.tile([P, V + C], F32, name="shared")
-        later = held.tile([P, V + C], F32, name="later")
+        names = ["d1_first", "d0_first", "d0_last", "d1_last"]
+        d1_first, d0_first, d0_last, d1_last = [held.tile([P, C], F32, name=name)[:] for name in names]
         for cols in chunks:
             nc.vector.tensor_tensor(m[:, cols], picked(0, cols), node[:, cols], ALU.max)
         for cols in chunks:
             nc.vector.tensor_tensor(h[:, cols], picked(1, cols), m[:, cols], ALU.max)
-        d1_first, d0, d1_last = shared[:, V - C // 2 : V + C // 2], later[:, :V], later[:, V:]
         nc.vector.tensor_tensor(d1_first, picked(1, first), h[:, first], ALU.subtract)
-        nc.vector.tensor_tensor(d0, picked(0, slice(0, V)), h[:], ALU.subtract)
+        nc.vector.tensor_tensor(d0_first, picked(0, first), h[:, first], ALU.subtract)
+        nc.vector.tensor_tensor(d0_last, picked(0, last), h[:, last], ALU.subtract)
         nc.vector.tensor_tensor(d1_last, picked(1, last), h[:, last], ALU.subtract)
 
-        negated = held.tile([P, V], F32, name="negated")
-        own_t = held.tile([P, V], F32, name="own_t")
-        parts = [first, slice(C, C + C // 2), slice(C + C // 2, V)]
         gaps = [psum.tile([P, C], F32, name=f"gap{c}") for c in range(len(chunks))]
-        opened = [psum.tile([P, cols.stop - cols.start], F32, name=f"opened{c}") for c, cols in enumerate(parts)]
+        opened = [psum.tile([P, C], F32, name=f"opened{c}") for c in range(len(chunks))]
+        negated = held.tile([P, V], F32, name="negated")
+        shared = held.tile([P, V], F32, name="shared")
+        own_t = [held.tile([P, C], F32, name=f"own{c}")[:] for c in range(len(chunks))]
+        level = held.tile([P, V], BF16, name="level")
+        lift = held.tile([P, V], F32, name="lift")
         for cols in chunks:
             nc.scalar.mul(negated[:, cols], node[:, cols], -1.0)
         for gap, cols in zip(gaps, chunks):
             add_transposed(gap, negated[:, cols], start=True, stop=False)
-        for gap, cols in zip(gaps, chunks):
-            add_transposed(gap, h[:, cols], start=False, stop=True)
-            nc.scalar.activation(own_t[:, cols], gap[:], ACT.Exp, scale=-1.0)
-        for bank, cols in zip(opened, parts):
-            add_transposed(bank, own_t[:, cols], start=True, stop=False)
-
-        e1_first, e0, e1_last = own_t[:, first], shared[:, :V], shared[:, V:]
-        nc.scalar.activation(e1_first, d1_first, ACT.Exp)
-        nc.scalar.activation(e0, d0, ACT.Exp)
-        nc.scalar.activation(e1_last, d1_last, ACT.Exp)
-
-        sums = held.tile([P, V], F32, name="sums")
-        on_tensor = [e1_first, e0[:, parts[1]], e1_last[:, C // 2 :]]
-        on_vector = [e0[:, first], e1_last[:, : C // 2], e0[:, parts[2]]]
-        for bank, cols, one, other in zip(opened, parts, on_tensor, on_vector):
-            nc.tensor.matmul(bank[:], identity[:], one, start=False, stop=True)
-            nc.vector.tensor_tensor(sums[:, cols], bank[:], other, ALU.add)
 
         pieces = [slice(c, c + W) for c in range(0, V, W)]
-        banks = ["opened0", "opened1", "free0", "free1", "free2", "gap0", "gap1", "opened2"]
+        banks = ["free0", "free1", "free2", "free3", "gap0", "gap1", "opened1", "opened0"]
         products = [psum.tile([P, W], F32, name=f"product{i}", tag=bank) for i, bank in enumerate(banks)]
-        logs = held.tile([P, V], F32, name="logs")
-        result = held.tile([P, V], F32, name="result")
-        x = held.tile([P, V], BF16, name="x", tag="shared")
         weights32 = held.tile([P, P], F32, name="weights32")
+        lowered = held.tile([P, P], BF16, name="lowered")
         nc.scalar.copy(weights32[:], weights[:])
-        for piece, product in zip(pieces[:EXACT], products):
-            nc.tensor.matmul(product[:], weights32[:], h[:, piece], start=True, stop=False)
-        for piece in pieces:
-            nc.scalar.activation(logs[:, piece], sums[:, piece], ACT.Ln)
-        for piece, product in zip(pieces[:EXACT], products):
-            nc.tensor.matmul(product[:], weights32[:], logs[:, piece], start=False, stop=True)
-        for piece, product in zip(pieces[EXACT:], products[EXACT:]):
-            nc.vector.tensor_tensor(x[:, piece], h[:, piece], logs[:, piece], ALU.add)
-            nc.tensor.matmul(product[:], weights[:], x[:, piece], start=True, stop=True)
-        for i, (piece, product) in enumerate(zip(pieces, products)):
-            if i < SCALAR_ALONE or i % 2 == 0:
-                nc.scalar.activation(result[:, piece], product[:], ACT.Relu, bias=bias[:, 0:1])
-            else:
-                nc.vector.tensor_scalar(result[:, piece], product[:], bias[:, 0:1], 0.0, ALU.add, ALU.max)
-            if i % 2 == 1:
-                nc.sync.dma_start(out[:, piece.start - W : piece.stop], result[:, piece.start - W : piece.stop])
+        nc.scalar.mul(lowered[:], weights[:], -BOUND)
+
+        def add_h(some):
+            for i in some:
+                nc.tensor.matmul(products[i][:], weights32[:], h[:, pieces[i]], start=True, stop=False)
+
+        def subtract_c(some):
+            for i in some:
+                nc.tensor.matmul(products[i][:], lowered[:], level[:, pieces[i]], start=False, stop=False)
+
+        add_h(range(0, 2))
+        nc.scalar.activation(level[:, first], h[:, first], ACT.Tanh, scale=1.0 / BOUND)
+        nc.scalar.activation(lift[:, first], level[:, first], ACT.Exp, scale=BOUND)
+        nc.scalar.activation(level[:, last], h[:, last], ACT.Tanh, scale=1.0 / BOUND)
+        for gap, own, cols in zip(gaps, own_t, chunks):
+            add_transposed(gap, h[:, cols], start=False, stop=True)
+            nc.scalar.activation(own, gap[:], ACT.Exp, scale=-1.0)
+        nc.scalar.activation(lift[:, last], level[:, last], ACT.Exp, scale=BOUND)
+        add_transposed(opened[0], own_t[0], start=True, stop=False)
+        add_transposed(opened[1], own_t[1], start=True, stop=True)
+        add_h(range(2, 4))
+
+        e1_first, e0_first = shared[:, first], shared[:, last]
+        e0_last = held.tile([P, C], F32, name="e0_last", tag="d1_first")[:]
+        e1_last = held.tile([P, C], F32, name="e1_last", tag="d0_first")[:]
+        nc.scalar.activation(e1_first, d1_first, ACT.Exp)
+        nc.scalar.activation(e0_first, d0_first, ACT.Exp)
+        nc.scalar.activation(e0_last, d0_last, ACT.Exp)
+        nc.scalar.activation(e1_last, d1_last, ACT.Exp)
+
+        nc.tensor.matmul(opened[0][:], identity[:], e1_first, start=False, stop=True)
+        add_h(range(4, 6))
+        subtract_c(range(0, 6))
+        partial = held.tile([P, V], F32, name="partial")
+        summed = held.tile([P, C], F32, name="summed")
+        lifted = held.tile([P, V], F32, name="lifted")
+        halves = [slice(0, C // 2), slice(C // 2, C)]
+        nc.vector.tensor_tensor(partial[:, last], opened[1][:], e0_last, ALU.add)
+        nc.vector.tensor_tensor(partial[:, first], opened[0][:], e0_first, ALU.add)
+        nc.vector.tensor_tensor(summed[:, halves[0]], partial[:, last][:, halves[0]], e1_last[:, halves[0]], ALU.add)
+        nc.vector.tensor_tensor(lifted[:, first], partial[:, first], lift[:, first], ALU.mult)
+        nc.vector.tensor_tensor(summed[:, halves[1]], partial[:, last][:, halves[1]], e1_last[:, halves[1]], ALU.add)
+        for half in halves:
+            nc.vector.tensor_tensor(lifted[:, last][:, half], summed[:, half], lift[:, last][:, half], ALU.mult)
+
+        for i in range(6, 8):
+            add_h([i])
+            subtract_c([i])
+
+        x = held.tile([P, V], BF16, name="x", tag="d1_last")
+        result = held.tile([P, V], F32, name="result", tag="lift")
+        for piece, product in zip(pieces, products):
+            nc.scalar.activation(x[:, piece], lifted[:, piece], ACT.Ln)
+            nc.tensor.matmul(product[:], weights[:], x[:, piece], start=False, stop=True)
+        for piece, product in zip(pieces, products):
+            nc.vector.tensor_scalar(result[:, piece], product[:], bias[:, 0:1], 0.0, ALU.add, ALU.max)
+            if piece.stop % (2 * W) == 0:
+                nc.sync.dma_start(out[:, piece.stop - 2 * W : piece.stop], result[:, piece.stop - 2 * W : piece.stop])

@@ -87,7 +87,7 @@ def tile_lookup_lse_relu_kernel(tc, tab, x0, w, b, offs, out):
             add_transposed(gap, negated[:, cols], start=True, stop=False)
 
         pieces = [slice(c, c + W) for c in range(0, V, W)]
-        banks = ["free0", "free1", "free2", "free3", "gap0", "gap1", "opened1", "opened0"]
+        banks = ["free0", "free1", "free2", "free3", "gap0", "gap1", "opened0", "opened1"]
         products = [psum.tile([P, W], F32, name=f"product{i}", tag=bank) for i, bank in enumerate(banks)]
         weights32 = held.tile([P, P], F32, name="weights32")
         lowered = held.tile([P, P], BF16, name="lowered")
@@ -102,23 +102,22 @@ def tile_lookup_lse_relu_kernel(tc, tab, x0, w, b, offs, out):
             for i in some:
                 nc.tensor.matmul(products[i][:], lowered[:], level[:, pieces[i]], start=False, stop=False)
 
-        add_h(range(0, 2))
         nc.scalar.activation(level[:, first], h[:, first], ACT.Tanh, scale=1.0 / BOUND)
         nc.scalar.activation(lift[:, first], level[:, first], ACT.Exp, scale=BOUND)
         nc.scalar.activation(level[:, last], h[:, last], ACT.Tanh, scale=1.0 / BOUND)
         for gap, own, cols in zip(gaps, own_t, chunks):
             add_transposed(gap, h[:, cols], start=False, stop=True)
             nc.scalar.activation(own, gap[:], ACT.Exp, scale=-1.0)
-        nc.scalar.activation(lift[:, last], level[:, last], ACT.Exp, scale=BOUND)
         add_transposed(opened[0], own_t[0], start=True, stop=False)
         add_transposed(opened[1], own_t[1], start=True, stop=True)
-        add_h(range(2, 4))
+        add_h(range(0, 4))
 
         e1_first, e0_first = shared[:, first], shared[:, last]
         e0_last = held.tile([P, C], F32, name="e0_last", tag="d1_first")[:]
         e1_last = held.tile([P, C], F32, name="e1_last", tag="d0_first")[:]
         nc.scalar.activation(e1_first, d1_first, ACT.Exp)
         nc.scalar.activation(e0_first, d0_first, ACT.Exp)
+        nc.scalar.activation(lift[:, last], level[:, last], ACT.Exp, scale=BOUND)
         nc.scalar.activation(e0_last, d0_last, ACT.Exp)
         nc.scalar.activation(e1_last, d1_last, ACT.Exp)
 
@@ -127,13 +126,13 @@ def tile_lookup_lse_relu_kernel(tc, tab, x0, w, b, offs, out):
         subtract_c(range(0, 6))
         partial = held.tile([P, V], F32, name="partial")
         summed = held.tile([P, C], F32, name="summed")
-        lifted = held.tile([P, V], F32, name="lifted")
+        lifted = held.tile([P, V], F32, name="lifted", tag="d1_last")
         halves = [slice(0, C // 2), slice(C // 2, C)]
-        nc.vector.tensor_tensor(partial[:, last], opened[1][:], e0_last, ALU.add)
         nc.vector.tensor_tensor(partial[:, first], opened[0][:], e0_first, ALU.add)
-        nc.vector.tensor_tensor(summed[:, halves[0]], partial[:, last][:, halves[0]], e1_last[:, halves[0]], ALU.add)
+        nc.vector.tensor_tensor(partial[:, last], opened[1][:], e0_last, ALU.add)
         nc.vector.tensor_tensor(lifted[:, first], partial[:, first], lift[:, first], ALU.mult)
-        nc.vector.tensor_tensor(summed[:, halves[1]], partial[:, last][:, halves[1]], e1_last[:, halves[1]], ALU.add)
+        for half in halves:
+            nc.vector.tensor_tensor(summed[:, half], partial[:, last][:, half], e1_last[:, half], ALU.add)
         for half in halves:
             nc.vector.tensor_tensor(lifted[:, last][:, half], summed[:, half], lift[:, last][:, half], ALU.mult)
 
@@ -141,7 +140,7 @@ def tile_lookup_lse_relu_kernel(tc, tab, x0, w, b, offs, out):
             add_h([i])
             subtract_c([i])
 
-        x = held.tile([P, V], BF16, name="x", tag="d1_last")
+        x = held.tile([P, V], BF16, name="x")
         result = held.tile([P, V], F32, name="result", tag="lift")
         for piece, product in zip(pieces, products):
             nc.scalar.activation(x[:, piece], lifted[:, piece], ACT.Ln)

@@ -113,8 +113,8 @@ def tile_lookup_lse_relu_kernel(tc, tab, x0, w, b, offs, out):
         add_h(range(0, 4))
 
         e1_first, e0_first = shared[:, first], shared[:, last]
-        e0_last = held.tile([P, C], F32, name="e0_last", tag="d1_first")[:]
-        e1_last = held.tile([P, C], F32, name="e1_last", tag="d0_first")[:]
+        e0_last = held.tile([P, C], F32, name="e0_last", tag="d0_first")[:]
+        e1_last = held.tile([P, C], F32, name="e1_last", tag="d1_first")[:]
         nc.scalar.activation(e1_first, d1_first, ACT.Exp)
         nc.scalar.activation(e0_first, d0_first, ACT.Exp)
         nc.scalar.activation(lift[:, last], level[:, last], ACT.Exp, scale=BOUND)
@@ -141,7 +141,7 @@ def tile_lookup_lse_relu_kernel(tc, tab, x0, w, b, offs, out):
             subtract_c([i])
 
         x = held.tile([P, V], BF16, name="x")
-        result = held.tile([P, V], F32, name="result", tag="lift")
+        result = held.tile([P, V], F32, name="result")
         for piece, product in zip(pieces, products):
             nc.scalar.activation(x[:, piece], lifted[:, piece], ACT.Ln)
             nc.tensor.matmul(product[:], weights[:], x[:, piece], start=False, stop=True)

@@ -61,6 +61,9 @@ def tile_lookup_lse_relu_kernel(tc, tab, x0, w, b, offs, out):
                 nc.tensor.matmul(bank[:, block], source[:, block], identity[:], is_transpose=True,
                                  start=start and k == 0, stop=stop and k == blocks - 1)
 
+        negated = held.tile([P, V], F32, name="negated")
+        nc.vector.tensor_scalar(negated[:, first], node[:, first], -1.0, None, ALU.mult)
+
         m = held.tile([P, V], F32, name="m")
         h = held.tile([P, V], F32, name="h")
         names = ["d1_first", "d0_first", "d0_last", "d1_last"]
@@ -76,13 +79,11 @@ def tile_lookup_lse_relu_kernel(tc, tab, x0, w, b, offs, out):
 
         gaps = [psum.tile([P, C], F32, name=f"gap{c}") for c in range(len(chunks))]
         opened = [psum.tile([P, C], F32, name=f"opened{c}") for c in range(len(chunks))]
-        negated = held.tile([P, V], F32, name="negated")
         shared = held.tile([P, V], F32, name="shared")
         own_t = [held.tile([P, C], F32, name=f"own{c}")[:] for c in range(len(chunks))]
         level = held.tile([P, V], BF16, name="level")
         lift = held.tile([P, V], F32, name="lift")
-        for cols in chunks:
-            nc.scalar.mul(negated[:, cols], node[:, cols], -1.0)
+        nc.scalar.mul(negated[:, last], node[:, last], -1.0)
         for gap, cols in zip(gaps, chunks):
             add_transposed(gap, negated[:, cols], start=True, stop=False)
 

import concourse.mybir as mybir

F32, BF16, U16 = mybir.dt.float32, mybir.dt.bfloat16, mybir.dt.uint16
ALU = mybir.AluOpType
ACT = mybir.ActivationFunctionType

P = 128
V = 1024
S = 2048
N = 2 * V
C = 512
Q = 32
PER = 16
SPLIT = (S - C) // 2
W = 128
BOUND = 32.0

FLOPS = 2 * P * P * V


def tile_lookup_lse_relu_kernel(tc, tab, x0, w, b, offs, out):
    nc = tc.nc
    with (
        tc.tile_pool(name="held", bufs=1) as held,
        tc.psum_pool(name="psum", bufs=1) as psum,
    ):
        first, last = slice(0, C), slice(C, V)
        chunks = [first, last]

        offsets = held.tile([P, N // PER], U16, name="offsets")
        table = held.tile([P, S], F32, name="table")
        node = held.tile([P, V], F32, name="node")
        weights = held.tile([P, P], BF16, name="weights")
        bias = held.tile([P, 1], F32, name="bias")
        nc.scalar.dma_start(table[:, SPLIT:], tab[:, SPLIT:])
        nc.sync.dma_start(node[:, first], x0[:, first])
        nc.sync.dma_start(offsets[:], offs)
        nc.sync.dma_start(table[:, :SPLIT], tab[:, :SPLIT])
        nc.sync.dma_start(node[:, last], x0[:, last])
        nc.sync.dma_start(weights[:], w)
        nc.sync.dma_start(bias[:], b)

        ones = held.tile([P, Q], F32, name="ones")
        column = held.tile([P, Q], F32, name="column", align_bytes=64)
        row = held.tile([P, Q], F32, name="row", align_bytes=64)
        identity = held.tile([P, P], F32, name="identity")
        nc.vector.memset(ones[:], 1.0)
        nc.vector.memset(identity[:], 0.0)
        nc.vector.tensor_tensor_scan(column[:], ones[:], ones[:], 0.0, ALU.mult, ALU.add)
        nc.vector.transpose(row[:], column[:])
        for q in range(0, P, Q):
            nc.vector.tensor_tensor(identity[q : q + Q, q : q + Q], column[q : q + Q, :], row[q : q + Q, :], ALU.is_equal)

        def picked(d, cols):
            return table[:].indirect(offsets[:, (d * V + cols.start) // PER : (d * V + cols.stop) // PER])

        def add_transposed(bank, source, start, stop):
            blocks = source.shape[1] // P
            for k in range(blocks):
                block = slice(k * P, (k + 1) * P)
                nc.tensor.matmul(bank[:, block], source[:, block], identity[:], is_transpose=True,
                                 start=start and k == 0, stop=stop and k == blocks - 1)

        negated = held.tile([P, V], F32, name="negated")
        nc.vector.tensor_scalar(negated[:, first], node[:, first], -1.0, None, ALU.mult)

        m = held.tile([P, V], F32, name="m")
        h = held.tile([P, V], F32, name="h")
        names = ["d1_first", "d0_first", "d0_last", "d1_last"]
        d1_first, d0_first, d0_last, d1_last = [held.tile([P, C], F32, name=name)[:] for name in names]
        for cols in chunks:
            nc.vector.tensor_tensor(m[:, cols], picked(0, cols), node[:, cols], ALU.max)
        for cols in chunks:
            nc.vector.tensor_tensor(h[:, cols], picked(1, cols), m[:, cols], ALU.max)
        nc.vector.tensor_tensor(d1_first, picked(1, first), h[:, first], ALU.subtract)
        nc.vector.tensor_tensor(d0_first, picked(0, first), h[:, first], ALU.subtract)
        nc.vector.tensor_tensor(d0_last, picked(0, last), h[:, last], ALU.subtract)
        nc.vector.tensor_tensor(d1_last, picked(1, last), h[:, last], ALU.subtract)

        gaps = [psum.tile([P, C], F32, name=f"gap{c}") for c in range(len(chunks))]
        opened = [psum.tile([P, C], F32, name=f"opened{c}") for c in range(len(chunks))]
        shared = held.tile([P, V], F32, name="shared")
        own_t = [held.tile([P, C], F32, name=f"own{c}")[:] for c in range(len(chunks))]
        level = held.tile([P, V], BF16, name="level")
        lift = held.tile([P, V], F32, name="lift")
        nc.scalar.mul(negated[:, last], node[:, last], -1.0)
        for gap, cols in zip(gaps, chunks):
            add_transposed(gap, negated[:, cols], start=True, stop=False)

        pieces = [slice(c, c + W) for c in range(0, V, W)]
        banks = ["free0", "free1", "free2", "free3", "gap0", "gap1", "opened0", "opened1"]
        products = [psum.tile([P, W], F32, name=f"product{i}", tag=bank) for i, bank in enumerate(banks)]
        weights32 = held.tile([P, P], F32, name="weights32")
        lowered = held.tile([P, P], BF16, name="lowered")
        nc.scalar.copy(weights32[:], weights[:])
        nc.scalar.mul(lowered[:], weights[:], -BOUND)

        def add_h(some):
            for i in some:
                nc.tensor.matmul(products[i][:], weights32[:], h[:, pieces[i]], start=True, stop=False)

        def subtract_c(some):
            for i in some:
                nc.tensor.matmul(products[i][:], lowered[:], level[:, pieces[i]], start=False, stop=False)

        nc.scalar.activation(level[:, first], h[:, first], ACT.Tanh, scale=1.0 / BOUND)
        nc.scalar.activation(lift[:, first], level[:, first], ACT.Exp, scale=BOUND)
        nc.scalar.activation(level[:, last], h[:, last], ACT.Tanh, scale=1.0 / BOUND)
        for gap, own, cols in zip(gaps, own_t, chunks):
            add_transposed(gap, h[:, cols], start=False, stop=True)
            nc.scalar.activation(own, gap[:], ACT.Exp, scale=-1.0)
        add_transposed(opened[0], own_t[0], start=True, stop=False)
        add_transposed(opened[1], own_t[1], start=True, stop=True)
        add_h(range(0, 4))

        e1_first, e0_first = shared[:, first], shared[:, last]
        e0_last = held.tile([P, C], F32, name="e0_last", tag="d0_first")[:]
        e1_last = held.tile([P, C], F32, name="e1_last", tag="d1_first")[:]
        nc.scalar.activation(e1_first, d1_first, ACT.Exp)
        nc.scalar.activation(e0_first, d0_first, ACT.Exp)
        nc.scalar.activation(lift[:, last], level[:, last], ACT.Exp, scale=BOUND)
        nc.scalar.activation(e0_last, d0_last, ACT.Exp)
        nc.scalar.activation(e1_last, d1_last, ACT.Exp)

        nc.tensor.matmul(opened[0][:], identity[:], e1_first, start=False, stop=True)
        add_h(range(4, 6))
        subtract_c(range(0, 6))
        partial = held.tile([P, V], F32, name="partial")
        summed = held.tile([P, C], F32, name="summed")
        lifted = held.tile([P, V], F32, name="lifted", tag="d1_last")
        halves = [slice(0, C // 2), slice(C // 2, C)]
        nc.vector.tensor_tensor(partial[:, first], opened[0][:], e0_first, ALU.add)
        nc.vector.tensor_tensor(partial[:, last], opened[1][:], e0_last, ALU.add)
        nc.vector.tensor_tensor(lifted[:, first], partial[:, first], lift[:, first], ALU.mult)
        for half in halves:
            nc.vector.tensor_tensor(summed[:, half], partial[:, last][:, half], e1_last[:, half], ALU.add)
        for half in halves:
            nc.vector.tensor_tensor(lifted[:, last][:, half], summed[:, half], lift[:, last][:, half], ALU.mult)

        for i in range(6, 8):
            add_h([i])
            subtract_c([i])

        x = held.tile([P, V], BF16, name="x")
        result = held.tile([P, V], F32, name="result")
        for piece, product in zip(pieces, products):
            nc.scalar.activation(x[:, piece], lifted[:, piece], ACT.Ln)
            nc.tensor.matmul(product[:], weights[:], x[:, piece], start=False, stop=True)
        for piece, product in zip(pieces, products):
            nc.vector.tensor_scalar(result[:, piece], product[:], bias[:, 0:1], 0.0, ALU.add, ALU.max)
            if piece.stop % (2 * W) == 0:
                nc.sync.dma_start(out[:, piece.stop - 2 * W : piece.stop], result[:, piece.stop - 2 * W : piece.stop])
